import numpy as np, ml_dtypes
CORES = [2,3,42,43,82,83,122,123]
N = 8
BF = ml_dtypes.bfloat16
V, HB, CH, LV, RO = 2048, 4096, 96, 3, 3
def places(w, dd):
    u = np.matmul(np.swapaxes(w, -1, -2), dd) & 4095
    return (((u * u) >> 5) + u) & (HB - 1)
def pattern(rng):
    return np.stack([np.tile(rng.integers(0, 256, a), 16 // a) for a in (int(v) for v in rng.choice(np.array([4, 8, 16]), 8))])
def near(rng, b, n):
    i = (np.arange(16)[:, None] + rng.integers(0, 16, (N, 8, 1, n))) % 16
    v = np.take_along_axis(np.broadcast_to(b[None, :, :, None], (N, 8, 16, n)), i, 2)
    s = rng.integers(1, 25, (N, 8, 1, n))
    return np.clip(v + np.rint(s * (2 * rng.random((N, 8, 16, n)) - 1)).astype(np.int64), 0, 255)
def parts(rng):
    b = pattern(rng); x = near(rng, b, V); x = np.where(rng.random((N, 8, 1, V)) < 0.1, rng.integers(0, 256, x.shape), x); c = near(rng, b, CH)
    h = rng.integers(0, V, (N, 8, 16, HB)); h[rng.random(h.shape) < 0.15] = V
    l = rng.integers(0, V, (N, 8, 16, V)); l[rng.random(l.shape) < 0.25] = V
    return x, h, l, c, rng.integers(0, 256, (8, 16, 16)), rng.integers(80, 400, (N, 8, 16))
def pack(x, h, l, c, w, t):
    return {"xr": np.ascontiguousarray(x.reshape(N, 128, V)).astype(np.float32).astype(BF), "hd": np.ascontiguousarray(h.reshape(N, 128, HB)).astype(np.int32),
            "nx": np.ascontiguousarray(l.reshape(N, 128, V)).astype(np.int32), "c0": np.ascontiguousarray(c.reshape(N, 128, CH)).astype(np.float32).astype(BF),
            "wt": np.tile(w.reshape(1, 128, 16), (N, 1, 1)).astype(np.float32).astype(BF), "th": np.ascontiguousarray(t.reshape(N, 128, 1)).astype(np.int32)}
def setup_inputs(rng):
    return pack(*parts(rng))
def setup_inputs_crowd(rng):
    x, h, l, c, w, t = parts(rng)
    c[:, ::2] = np.take_along_axis(c, rng.integers(0, 5, (N, 8, 1, CH)), 3)[:, ::2]
    few = np.concatenate([np.array([0, V - 1]), 1 + rng.permutation(V - 2)[:30]])
    h[:, 1::2] = rng.choice(few, (N, 4, 16, HB))
    return pack(x, h, l, c, w, t)
def setup_inputs_ties(rng):
    x, h, l, c, w, t = parts(rng)
    t = rng.choice(np.array([0, 1, 15, 16, 17, 100, 250, 400]), (N, 8, 16)); x[:, ::2] = rng.integers(0, 256, (N, 4, 16, V))
    e = rng.integers(0, 2, (N, 2, 16, 1)) == 1; a = rng.integers(0, 16, (N, 2, 16, CH)); b = rng.integers(0, 16, (N, 2, 16, V))
    c[:, 2::4] = np.roll(np.where(e, 255 - a, a), 1, axis=2); x[:, 2::4] = np.where(e, b, 255 - b); t[:, 2::4] = rng.integers(1500, 3501, (N, 2, 16))
    dd = np.roll(c, -1, axis=2); k = places(w[None], dd); cc = np.arange(CH)
    for q in range(N):
        for g in range(8):
            o = rng.permutation(V)[:8 * CH].reshape(CH, 8); ds = np.argsort(rng.random((CH, 16)), axis=1)[:, :8]; hg, lg, xg, dg = h[q, g], l[q, g], x[q, g], dd[q, g]
            for j in range(8):
                d = ds[:, j]; rd = o[:, j]; at = k[q, g][d, cc]
                if j < 4: hg[d, at] = rd
                else:
                    e = hg[d, at]
                    if LV == 3 and j >= 6: e = np.where(e < V, lg[d, np.minimum(e, V - 1)], V)
                    m = e < V; lg[d[m], e[m]] = rd[m]
                far = np.maximum(t[q, g][d] + rng.integers(-1, 2, CH), 0)
                z = np.minimum(rng.integers(0, 9, (16, CH)), (far // 16)[None, :])
                step = (far // 16)[None, :] + (np.argsort(rng.random((16, CH)), axis=0) < (far % 16)[None, :]) + z - np.roll(z, 1, axis=0)
                xg[:, rd] = dg + np.where(dg < 128, 1, -1) * step
    return pack(x, h, l, c, w, t)
def setup_inputs_ends(rng):
    x, h, l, c, w, t = parts(rng); m = V // 2
    h[:, 0, :15] = V
    l[:, 1] = V
    x[:, 2:4, :, :m] = rng.integers(0, 256, (N, 2, 16, m)); h[:, 2:4] = rng.integers(0, m, (N, 2, 16, HB)); l[:, 2:4] = rng.integers(m, V, (N, 2, 16, V)); l[:, 3, :15] = V
    h[:, 4] = rng.choice(np.array([0, V - 1, V]), (N, 16, HB)); h[:, 4, 0] = 0; h[:, 4, 1] = V - 1; l[:, 4, :, 0] = V - 1; l[:, 4, :, V - 1] = 0
    x[:, 4, :, 0] = np.roll(c[:, 4, :, 0], -1, axis=1); x[:, 4, :, V - 1] = np.roll(c[:, 4, :, CH - 1], -1, axis=1)
    h[:, 5] = V
    l[:, 6] = np.arange(V)
    return pack(x, h, l, c, w, t)
def setup_inputs_eager(rng):
    x, h, l, c, w, t = parts(rng)
    x = rng.integers(0, 256, x.shape); c = rng.integers(0, 256, c.shape); t[:] = 4080
    x[:, 0] = 255 * rng.integers(0, 2, (N, 1, V)); c[:, 0] = 255 * rng.integers(0, 2, (N, 1, CH)); t[:, 0] = 4079 + rng.integers(0, 2, (N, 16))
    w[0] = 255; w[1] = 0; w[2] = rng.choice(np.array([0, 1, 255]), (16, 16)); t[:, 3] = 4079
    return pack(x, h, l, c, w, t)
def setup_inputs_spread(rng):
    x, h, l, c, w, t = parts(rng)
    x = np.minimum((np.exp2(8 * rng.random((N, 8, 1, V))) * rng.random((N, 8, 16, V))).astype(np.int64), 255)
    c = np.minimum((np.exp2(8 * rng.random((N, 8, 1, CH))) * rng.random((N, 8, 16, CH))).astype(np.int64), 255)
    w = np.minimum((np.exp2(8 * rng.random((8, 1, 16))) * (0.5 + 0.5 * rng.random((8, 16, 16)))).astype(np.int64), 255)
    t = np.minimum(np.exp2(12 * rng.random((N, 8, 16))).astype(np.int64), 4080)
    p = 1 + 2 * rng.random((N, 8, 16, 1))
    h = np.where(h == V, V, np.minimum((V * rng.random(h.shape) ** p).astype(np.int64), V - 1))
    l = np.where(l == V, V, np.minimum((V * rng.random(l.shape) ** p).astype(np.int64), V - 1))
    return pack(x, h, l, c, w, t)
def check_inputs(d):
    bad = []
    for k, lo, hi in (("xr", 0, 255), ("hd", 0, V), ("nx", 0, V), ("c0", 0, 255), ("wt", 0, 255), ("th", 0, 4080)):
        v = np.asarray(d[k]).astype(np.float64)
        if not bool(np.all((v >= lo) & (v <= hi))): bad.append("range of " + k)
        elif bool(np.any(v != np.floor(v))): bad.append("whole numbers in " + k)
    v = np.asarray(d["wt"]).astype(np.float64)
    if bool(np.any(v != v[:1])): bad.append("wt alike on all ranks")
    return bad
def reference(xr, hd, nx, c0, wt, th):
    x = np.concatenate([xr.astype(np.float32).astype(np.int64).reshape(N, 8, 16, V), np.full((N, 8, 16, 1), 512, np.int64)], axis=3)
    h = hd.astype(np.int64).reshape(N, 8, 16, HB); l = np.concatenate([nx.astype(np.int64).reshape(N, 8, 16, V), np.full((N, 8, 16, 1), V, np.int64)], axis=3)
    c = c0.astype(np.float32).astype(np.int64).reshape(N, 8, 16, CH); w = wt.astype(np.float32).astype(np.int64).reshape(N, 8, 16, 16)
    lim = np.tile(th.astype(np.int64).reshape(N, 8, 16), (1, 1, LV))[..., None]; low = np.tri(CH, k=-1, dtype=bool); took = np.zeros((N, 8, RO, CH), np.int64)
    for t in range(RO):
        dd = np.roll(c, -1, axis=2)
        cand = [np.take_along_axis(h, places(w, dd), 3)]
        for i in range(1, LV): cand.append(np.take_along_axis(l, cand[-1], 3))
        cd = np.concatenate(cand, axis=2)
        v = np.take_along_axis(x, cd.reshape(N, 8, 1, 16 * LV * CH), 3).reshape(N, 8, 16, 16 * LV, CH)
        good = np.add.reduce(np.abs(v - dd[:, :, :, None, :]), axis=2) <= lim
        first = np.argmax(good, axis=2)[:, :, None, :]
        rd = np.where(np.any(good, axis=2), np.take_along_axis(cd, first, 2)[:, :, 0], V)
        lost = np.any((rd[..., :, None] == rd[..., None, :]) & low, axis=-1)
        win = (rd < V) & ~lost; rd = np.where(win, rd, V); took[:, :, t] = rd
        c = np.where(win[:, :, None, :], (3 * dd + np.take_along_axis(x, rd[:, :, None, :], 3)) >> 2, dd)
        np.put_along_axis(x, rd[:, :, None, :], 512, 3)
        c = np.roll(c, 1 + t % (N - 1), axis=0)
    return {"yc": c.reshape(N, 128, CH).astype(np.float32), "yt": took.reshape(N, 8, RO * CH).astype(np.float32)}

@@ -1,0 +1,620 @@
+from concourse.mybir import AluOpType as ALU, ActivationFunctionType as ACT
+
+V, HB, CH, RO, N = 2048, 4096, 96, 3, 8
+XW = V + 112
+CFG = {
+    "streams": [(0, 48), (48, 96)],
+    "banks": [(("ps0", 0), ("ps1", 0), ["ps4", "ps5"]), (("ps2", 0), ("ps3", 0), ["ps6", "ps7"])],
+    "le": [[['sv', 'sv', 'vs'], ['vv', 'vs', 's']], [['sv', 'vs', 's'], ['vs', 'vs', 'vs']], [['vs', 's', 'sv'], ['sv', 'vs', 'vs']]],
+    "xe": [[['sv', 'vs', 'vv'], ['sv', 'vv', 'vv']], [['vs', 'vv', 'vv'], ['sv', 'vs', 'vv']], [['vv', 'sv', 'vv'], ['sv', 'sv', 'vv']]],
+    "how": [[['pe', 'pe', 'abs'], ['pe', 'pe', 'abs']], [['pe', 'pe', 'abs'], ['pe', 'pe', 'abs']], [['abs', 'pe', 'abs'], ['pe', 'pe', 'abs']]],
+    "bias": [[-2000, -2000], [1000, 0], [1000, 0]],
+    "split": True,
+    "tomb_s": True,
+    "xfirst": False,
+    "seed": 595, "tries": 4,
+}
+MAXS = 2
+
+SCRATCH = {
+    "hdw": ("sbuf", [128, HB], "int32"), "nxw": ("sbuf", [128, V + 8], "int32"),
+    "xw": ("sbuf", [128, XW], "bfloat16"),
+    "c0b": ("sbuf", [128, CH], "bfloat16"), "wtb": ("sbuf", [128, 16], "bfloat16"),
+    "thi": ("sbuf", [128, 4], "int32"), "thf": ("sbuf", [128, 4], "float32"),
+    "dcol": ("sbuf", [128, 128], "float32"), "gcol": ("sbuf", [128, 128], "float32"),
+    "pi": ("sbuf", [128, 8], "int32"), "pf": ("sbuf", [128, 8], "float32"),
+    "blk": ("sbuf", [128, 128], "float32"), "deq": ("sbuf", [128, 128], "float32"),
+    "tmpa": ("sbuf", [128, 128], "float32"), "tmpb": ("sbuf", [128, 128], "float32"), "tmpc": ("sbuf", [128, 128], "float32"),
+    "tmpd": ("sbuf", [128, 128], "float32"),
+    "rot": ("sbuf", [128, 128], "bfloat16"), "rott": ("sbuf", [128, 128], "bfloat16"), "wsh": ("sbuf", [128, 128], "bfloat16"),
+    "idb": ("sbuf", [128, 128], "bfloat16"), "nidb": ("sbuf", [128, 128], "bfloat16"),
+    "idh": ("sbuf", [128, 128], "float16"), "nidh": ("sbuf", [128, 128], "float16"),
+    "oneh": ("sbuf", [128, 128], "float16"), "kblk": ("sbuf", [128, 128], "bfloat16"),
+    "trih": ("sbuf", [128, 128], "float16"), "o4h": ("sbuf", [128, 128], "float16"),
+    "ed": ("sbuf", [128, 2048], "float16"),
+    "b1": ("sbuf", [128, 144], "bfloat16"), "b2": ("sbuf", [128, 144], "bfloat16"), "bn": ("sbuf", [128, 144], "bfloat16"),
+    "rio": ("sbuf", [128, 1024], "bfloat16"), "rr": ("sbuf", [128, 1024], "bfloat16"),
+    "nmask": ("sbuf", [128, CH], "float32"), "maskc": ("sbuf", [128, CH], "float32"), "maskd": ("sbuf", [128, CH], "float32"),
+    "placec": ("sbuf", [128, CH], "float32"), "placed": ("sbuf", [128, CH], "float32"),
+    "bc": ("sbuf", [128, 8], "float32"),
+    "g8": ("sbuf", [128, 8], "float32"), "g8n": ("sbuf", [128, 8], "float32"),
+    "c512": ("sbuf", [128, CH], "bfloat16"),
+    "landd": ("sbuf", [128, 2 * CH], "bfloat16"), "lande": ("sbuf", [128, 2 * CH], "bfloat16"), "landf": ("sbuf", [128, CH], "float32"),
+    "dsb": ("sbuf", [128, RO * CH], "bfloat16"), "dtb": ("sbuf", [128, 128 * MAXS], "bfloat16"),
+    "h1": ("sbuf", [128, CH], "int32"), "h2": ("sbuf", [128, CH], "int32"), "h3": ("sbuf", [128, CH], "int32"),
+    "h4": ("sbuf", [128, CH], "int32"), "h5": ("sbuf", [128, CH], "int32"), "hu": ("sbuf", [128, CH], "uint16"),
+    "off": ("sbuf", [128, 3 * CH], "uint16"), "cand": ("sbuf", [128, 3 * CH], "float16"),
+    "gl0": ("sbuf", [128, 16 * CH], "float16"), "gl1": ("sbuf", [128, 16 * CH], "float16"), "gl2": ("sbuf", [128, 16 * CH], "float16"),
+    "gx0": ("sbuf", [128, 16 * CH], "bfloat16"), "gx1": ("sbuf", [128, 16 * CH], "bfloat16"), "gx2": ("sbuf", [128, 16 * CH], "bfloat16"),
+    "zz0": ("sbuf", [128, 16 * CH], "bfloat16"), "zz1": ("sbuf", [128, 16 * CH], "bfloat16"), "zz2": ("sbuf", [128, 16 * CH], "bfloat16"),
+    "drep": ("sbuf", [128, 16 * CH], "bfloat16"),
+    "near": ("sbuf", [128, 3 * CH], "float16"), "yy": ("sbuf", [128, 3 * CH], "float16"),
+    "mm": ("sbuf", [128, CH], "float32"), "hold": ("sbuf", [128, CH], "float32"), "mq": ("sbuf", [128, CH], "float32"),
+    "hold2": ("sbuf", [128, CH], "float32"),
+    "m2": ("sbuf", [128, RO * CH], "float32"), "offw": ("sbuf", [128, 8 * MAXS], "uint16"), "offt": ("sbuf", [128, 8 * MAXS], "uint16"),
+    "offf": ("sbuf", [128, 8], "float32"), "junk": ("sbuf", [128, CH], "float32"),
+    "ee": ("sbuf", [128, 4 * CH], "bfloat16"), "zs": ("sbuf", [128, CH], "bfloat16"), "dl": ("sbuf", [128, CH], "int32"),
+    "ww": ("sbuf", [128, CH], "bfloat16"), "dw": ("sbuf", [128, RO * CH], "bfloat16"), "cn": ("sbuf", [128, 2 * CH], "bfloat16"),
+    "cf": ("sbuf", [128, CH], "float32"), "yts": ("sbuf", [128, RO * CH], "float32"),
+}
+for b in range(8):
+    SCRATCH["ps%d" % b] = ("psum", [128, 512], "float32")
+SEMAPHORES = ["qv", "qs", "qt", "qg", "sent"] + ["d%d" % i for i in range(16)] + ["a%d" % i for i in range(6 * MAXS)]
+BYTES = {"float32": 4, "int32": 4, "bfloat16": 2, "float16": 2, "uint16": 2}
+
+
+def R(name, c0=0, c1=None, step=1, p0=0, p1=128):
+    if c1 is None:
+        c1 = SCRATCH[name][1][1]
+    return ("r", name, p0, p1, c0, c1, step)
+
+
+def IND(win, off):
+    return ("i", win, off)
+
+
+def isref(a):
+    return isinstance(a, tuple) and len(a) > 0 and a[0] in ("r", "i", "d")
+
+
+def cols(r):
+    if r[0] == "i":
+        return 16 * cols(r[2])
+    return len(range(r[4], r[5], r[6]))
+
+
+def width(r):
+    return BYTES[SCRATCH[(r[1] if r[0] == "r" else r[1][1])][2]]
+
+
+def build():
+    ops, log, tag = [], {}, [0]
+    STREAMS = CFG["streams"]
+    NS = len(STREAMS)
+
+    def add(eng, ins, cost, kind="c", after=(), extra=None):
+        rd, wr = [], []
+        for m, args, kw in ins:
+            refs = [(i == 0, a) for i, a in enumerate(args) if isref(a)] + [(k == "accum_out", a) for k, a in kw.items() if isref(a)]
+            for out, a in refs:
+                if kind == "rdma" and out:
+                    continue
+                if a[0] == "i":
+                    rd.append(a[2])
+                    (wr if out else rd).append(a[1])
+                elif a[0] == "r":
+                    (wr if out else rd).append(a)
+        me = len(ops)
+        deps = {}
+        for isw, lst in ((False, rd), (True, wr)):
+            for a in lst:
+                for o, ow, b in log.get(a[1], []):
+                    if (isw or ow) and a[2] < b[3] and b[2] < a[3] and a[4] < b[5] and b[4] < a[5]:
+                        deps[o] = "ord" if (eng == "t" and ops[o]["eng"] == "t") else "raw"
+        for o in after:
+            deps.setdefault(o, "ord")
+        for isw, lst in ((False, rd), (True, wr)):
+            for a in lst:
+                if isw and a[6] == 1:
+                    log[a[1]] = [x for x in log.get(a[1], []) if not (a[2] <= x[2][2] and x[2][3] <= a[3] and a[4] <= x[2][4] and x[2][5] <= a[5])]
+                log.setdefault(a[1], []).append((me, isw, a))
+        banks = sorted({a[1] for a in rd + wr if a[1].startswith("ps")})
+        ops.append({"bias": tag[0], "eng": eng, "ins": ins, "cost": cost, "kind": kind, "deps": deps, "banks": banks, "x": extra})
+        return me
+
+    def vec(m, *args, **kw):
+        refs = [a for a in args if isref(a)]
+        n = cols(args[0])
+        if args[0][0] == "i":
+            cost = ("sc", n)
+        elif any(a[0] == "i" for a in refs):
+            cost = ("g", n)
+        else:
+            big = [a for a in refs if cols(a) == n]
+            f = 0.5 if all(width(a) == 2 for a in big) else 1.0
+            if m == "tensor_tensor":
+                f = 1.0 if any(a[1].startswith("ps") for a in big[1:]) else 2.0
+            cost = ("v", n * f)
+        return add("v", [(m, args, kw)], cost)
+
+    def ts(out, a, s1, op0, s2=None, op1=None):
+        return vec("tensor_scalar", out, a, s1, s2, op0) if op1 is None else vec("tensor_scalar", out, a, s1, s2, op0, op1)
+
+    def tt(out, a, b, op):
+        return vec("tensor_tensor", out, a, b, op)
+
+    def act(out, a, f, **kw):
+        return add("s", [("activation", (out, a, f), kw)], ("g" if a[0] == "i" else "s", cols(a)))
+
+    def copy(e, out, a):
+        return vec("tensor_copy", out, a) if e == "v" else act(out, a, ACT.Copy)
+
+    def mms(lst):
+        ins, c = [], 0
+        for i, (o, l, r) in enumerate(lst):
+            ins.append(("matmul", (o, l, r, i == 0, i == len(lst) - 1), {}))
+            c += max(min(64, cols(l)), cols(r)) * (4 if width(l) == 4 else 1)
+        return add("t", ins, ("t", c, len(lst)))
+
+    nd = [0]
+
+    def dma(q, out, in_, nbytes, after=()):
+        nd[0] += 1
+        return add(q, [("dma_start", (out, in_), {})], ("dma", nbytes), "dma", after, "d%d" % (nd[0] - 1))
+
+    na = [0]
+
+    def send(t, dst, src):
+        sem = "a%d" % na[0]
+        na[0] += 1
+        o = add("g", [("remote", (dst, src), {})], ("r",), "rdma", (), (t, sem))
+        return add(None, [("arrive", (dst,), {})], ("a",), "arr", (o,), (t, sem))
+
+    a = dma("y", R("c0b"), ("d", "c0", None), 24576)
+    a = dma("y", R("hdw"), ("d", "hd", None), 128 * HB * 4, (a,))
+    rest = [(R("nxw", 0, V), ("d", "nx", None), 128 * V * 4), (R("xw", 0, V), ("d", "xr", None), 128 * V * 2)]
+    if CFG["xfirst"]:
+        rest.reverse()
+    for o, i, n in rest:
+        a = dma("y", o, i, n, (a,))
+    a = dma("s", R("wtb"), ("d", "wt", None), 4096)
+    a = dma("s", R("thi", 0, 1), ("d", "th", None), 512, (a,))
+    W = 16 * max(b - a for a, b in STREAMS)
+    hows = {x for a in CFG["how"] for b in a for x in b}
+    imp = {"allow_small_or_imprecise_dtypes": True}
+    add("g", [("iota", (R("pi", 0, 1), [[0, 1]], 0, 1), {})], ("io", 1))
+    add("g", [("iota", (R("gcol"), [[1, 8], [0, 16]], 0, 0), imp)], ("io", 128))
+    add("g", [("iota", (R("dcol"), [[0, 8], [1, 16]], 0, 0), imp)], ("io", 128))
+    add("g", [("iota", (R("rio", 0, W), [[1, W // 16], [0, 16]], 0, -1), imp)], ("io", W))
+    ts(R("pi", 1, 2), R("pi", 0, 1), 4, ALU.arith_shift_right)
+    ts(R("pi", 2, 3), R("pi", 0, 1), 15, ALU.bitwise_and)
+    vec("tensor_copy", R("pf", 1, 3), R("pi", 1, 3))
+    pg, pd = R("pf", 1, 2), R("pf", 2, 3)
+    ts(R("blk"), R("gcol"), pg, ALU.is_equal)
+    ts(R("deq"), R("dcol"), pd, ALU.is_equal)
+    vec("tensor_copy", R("tmpa", 0, 127), R("deq", 1, 128))
+    vec("tensor_copy", R("tmpa", 127, 128), R("deq", 0, 1))
+    tt(R("rot"), R("tmpa"), R("blk"), ALU.mult)
+    vec("tensor_copy", R("tmpc", 1, 128), R("deq", 0, 127))
+    vec("tensor_copy", R("tmpc", 0, 1), R("deq", 127, 128))
+    tt(R("rott"), R("tmpc"), R("blk"), ALU.mult)
+    mms([(R("ps7", 0, 16), R("rott"), R("wtb"))])
+    for gq in range(8):
+        ts(R("wsh", 16 * gq, 16 * gq + 16), R("ps7", 0, 16), R("blk", 16 * gq, 16 * gq + 1), ALU.mult)
+    tt(R("idh"), R("deq"), R("blk"), ALU.mult)
+    for d in range(16):
+        ts(R("ed", 128 * d, 128 * d + 128), R("idh"), R("deq", d, d + 1), ALU.mult)
+    ts(R("nidb"), R("idh"), -1.0, ALU.mult)
+    ts(R("nidh"), R("idh"), -1.0, ALU.mult)
+    vec("tensor_copy", R("idb"), R("idh"))
+    vec("tensor_copy", R("oneh"), R("blk"))
+    ts(R("kblk"), R("oneh"), 1024.0, ALU.mult)
+    ts(R("o4h"), R("oneh"), -4096.0, ALU.mult)
+    ts(R("tmpb"), R("dcol"), pd, ALU.is_gt)
+    tt(R("tmpd"), R("tmpb"), R("deq"), ALU.subtract)
+    tt(R("trih"), R("tmpd"), R("o4h"), ALU.mult)
+    bs = [("b1", 1.0)] if hows & {"pe", "abs"} else []
+    if "relu" in hows:
+        bs += [("b2", 2.0), ("bn", -1.0)]
+    for nm, f in bs:
+        vec("memset", R(nm), 0.0)
+        ts(R(nm, 15, 128, 16), R("blk", 0, 128, 16), f, ALU.mult)
+    ts(R("rr", 0, W), R("rio", 0, W), 0.0, ALU.is_equal)
+    mask = "deq"
+    ts(R("nmask"), R(mask, 0, CH), -1.0, ALU.mult, 1.0, ALU.add)
+    ts(R("pf", 3, 4), pd, 1.0, ALU.add)
+    ts(R("placec"), R("gcol", 0, CH), 16.0, ALU.mult, R("pf", 3, 4), ALU.add)
+    ts(R("placed"), R("placec"), float(V), ALU.add)
+    ts(R("bc", 0, 6), R("placed", 0, CH, 16), 0.0625 if CFG["tomb_s"] else 1.0, ALU.mult)
+    tt(R("maskc"), R("placec"), R(mask, 0, CH), ALU.mult)
+    tt(R("maskd"), R("placed"), R(mask, 0, CH), ALU.mult)
+    vec("tensor_copy", R("g8"), R("blk", 0, 128, 16))
+    ts(R("g8n"), R("g8"), -1.0, ALU.mult)
+    vec("memset", R("c512"), 512.0)
+    vec("memset", R("xw", V, XW), 512.0)
+    vec("memset", R("nxw", V, V + 8), V)
+    vec("tensor_copy", R("thf", 0, 1), R("thi", 0, 1))
+
+    xwin = R("xw")
+    for t in range(RO):
+        for s, (c0, c1) in enumerate(STREAMS):
+            nc = c1 - c0
+            tag[0] = CFG["bias"][t][s]
+            (Pb, p0), (Qb, q0), zb = CFG["banks"][s]
+            NZ = len(zb)
+            src = [R("c0b", c0, c1)] if t == 0 else [R("landd", (t - 1) * CH + c0, (t - 1) * CH + c1)]
+            if t > 0 and CFG["split"]:
+                src.append(R("lande", (t - 1) * CH + c0, (t - 1) * CH + c1))
+            D = R("dsb", t * CH + c0, t * CH + c1)
+            DT = R("dtb", 128 * s, 128 * s + 128, 1, 0, nc)
+            ph = R(Pb, p0, p0 + nc)
+            mms([(ph, R("wsh"), x) for x in src])
+            pD, pDT = R(Qb, q0, q0 + nc), R(Qb, q0 + 3 * nc, q0 + 3 * nc + 128, 1, 0, nc)
+            mms([(pDT, x, R("rot")) for x in src])
+            mms([(pD, R("rot"), x) for x in src])
+            act(DT, pDT, ACT.Copy)
+            act(D, pD, ACT.Copy)
+            if CFG["split"] and t < RO - 1:
+                send(t, R("landd", t * CH + c0, t * CH + c1), D)
+            h = [R("h%d" % i, c0, c1) for i in range(1, 6)]
+            vec("tensor_copy", h[0], ph)
+            ts(h[1], h[0], HB - 1, ALU.bitwise_and)
+            ts(h[2], h[1], 32.0, ALU.add)
+            tt(h[3], h[1], h[2], ALU.mult)
+            ts(h[4], h[3], 5, ALU.arith_shift_right, HB - 1, ALU.bitwise_and)
+            lb, l0 = "hu", c0
+            vec("tensor_copy", R(lb, c0, c1), h[4])
+            w0, ck = 16 * c0, 16 * nc // NZ
+            if any(x != "pe" for x in CFG["how"][t][s]):
+                for i in range(NZ):
+                    mms([(R(zb[i], 0, ck), DT, R("rr", i * ck, (i + 1) * ck, 1, 0, nc))])
+                    act(R("drep", w0 + i * ck, w0 + (i + 1) * ck), R(zb[i], 0, ck), ACT.Copy)
+            for l in range(3):
+                gl, gx, zz = "gl%d" % l, "gx%d" % l, "zz%d" % l
+                le = CFG["le"][t][s][l]
+                n = nc // len(le)
+                for i, e in enumerate(le):
+                    copy(e, R(gl, w0 + 16 * n * i, w0 + 16 * n * (i + 1)), IND(R("hdw") if l == 0 else R("nxw"), R(lb, l0 + n * i, l0 + n * (i + 1))))
+                pa = R(Pb, p0 + (1 + l) * nc, p0 + (2 + l) * nc)
+                mms([(pa, R("ed", 128 * d, 128 * d + 128), R(gl, w0 + d, w0 + 16 * nc, 16)) for d in range(16)])
+                lb, l0 = "off", 3 * c0 + l * nc
+                vec("tensor_copy", R(lb, l0, l0 + nc), pa)
+                how, xe = CFG["how"][t][s][l], CFG["xe"][t][s][l]
+                n = nc // len(xe)
+                for i, e in enumerate(xe):
+                    G, a = R(gx, w0 + 16 * n * i, w0 + 16 * n * (i + 1)), IND(xwin, R(lb, l0 + n * i, l0 + n * (i + 1)))
+                    if how == "pe":
+                        copy(e, G, a)
+                    else:
+                        tt(G, a, R("drep", G[4], G[5]), ALU.subtract)
+                        Z = R(zz, G[4], G[5])
+                        if how == "abs":
+                            act(Z, G, ACT.Abs)
+                        else:
+                            ts(Z, G, 0.0, ALU.max)
+                if how == "pe":
+                    for i in range(NZ):
+                        pz = R(zb[i], 0, ck)
+                        mms([(pz, DT, R("rr", i * ck, (i + 1) * ck, 1, 0, nc)), (pz, R("nidb"), R(gx, w0 + i * ck, w0 + (i + 1) * ck))])
+                        act(R(zz, w0 + i * ck, w0 + (i + 1) * ck), pz, ACT.Abs)
+                pq = R(Qb, q0 + l * nc, q0 + (l + 1) * nc)
+                parts = (("bn", gx), ("b2", zz)) if how == "relu" else (("b1", zz),)
+                mms([(pq, R(bn, 15 - d, 143 - d), R(bf, w0 + d, w0 + 16 * nc, 16)) for bn, bf in parts for d in range(16)])
+            n0 = 3 * c0
+            cand = R("cand", n0, n0 + 3 * nc)
+            vec("tensor_copy", cand, R("off", n0, n0 + 3 * nc))
+            ts(R("near", n0, n0 + 3 * nc), R(Qb, q0, q0 + 3 * nc), R("thf", 0, 1), ALU.is_le)
+            pv = R(Qb, q0 + 3 * nc, q0 + 6 * nc)
+            mms([(pv, R("nidh"), cand),
+                 (R(Qb, q0 + 4 * nc, q0 + 6 * nc), R("o4h"), R("near", n0, n0 + 2 * nc)),
+                 (R(Qb, q0 + 5 * nc, q0 + 6 * nc), R("o4h"), R("near", n0, n0 + nc)),
+                 (pv, R("trih"), R("near", n0, n0 + 3 * nc))])
+            ts(R("yy", n0, n0 + 3 * nc), pv, -float(V), ALU.add, 0.0, ALU.max)
+            mms([(R(Qb, q0 + 6 * nc, q0 + 7 * nc), R("oneh"), R("yy", n0 + l * nc, n0 + (l + 1) * nc)) for l in range(3)])
+        for s, (c0, c1) in enumerate(STREAMS):
+            nc = c1 - c0
+            tag[0] = CFG["bias"][t][s]
+            K, k0 = nc // 16, c0 // 16
+            (Pb, p0), (Qb, q0), zb = CFG["banks"][s]
+            D = R("dsb", t * CH + c0, t * CH + c1)
+            pq = R(Qb, q0 + 6 * nc, q0 + 7 * nc)
+            m, hold = R("mm", c0, c1), R("hold", c0, c1)
+            tt(m, R(mask, 0, nc), pq, ALU.mult)
+            vec("tensor_tensor_scan", hold, R("nmask", 0, nc), m, 0.0, ALU.mult, ALU.add)
+            ow = R("offw", 8 * s, 8 * s + K)
+            ts(ow, R("hold", c0 + 15, c1, 16), -1.0, ALU.mult, float(V), ALU.add)
+            z = R("zs", c0, c1)
+            tt(z, IND(xwin, ow), D, ALU.subtract)
+            pl = [(R(Pb, p0, p0 + nc), R("idb"), z)]
+            for k in range(K):
+                n = nc - 16 * k - 1
+                e = R("ee", 4 * c0 + k * nc, 4 * c0 + k * nc + n)
+                tt(e, R("hold", c0, c0 + n), R(Qb, q0 + 7 * nc - n, q0 + 7 * nc), ALU.is_equal)
+                pl.append((R(Pb, p0 + nc - n, p0 + nc), R("kblk"), e))
+            ts(R("dl", c0, c1), z, 0.25, ALU.mult, -0.375, ALU.add)
+            mms(pl)
+            w = R("ww", c0, c1)
+            ts(w, R(Pb, p0, p0 + nc), 256.0, ALU.is_lt)
+            dw = R("dw", t * CH + c0, t * CH + c1)
+            tt(dw, R("dl", c0, c1), w, ALU.mult)
+            if t == RO - 1:
+                tt(R("cf", c0, c1), dw, D, ALU.add)
+                send(t, R("landf", c0, c1), R("cf", c0, c1))
+                dma("y", ("d", "yc", (c0, c1)), R("landf", c0, c1), 128 * nc * 4)
+            elif CFG["split"]:
+                send(t, R("lande", t * CH + c0, t * CH + c1), dw)
+            else:
+                cn = R("cn", t * CH + c0, t * CH + c1)
+                tt(cn, dw, D, ALU.add)
+                send(t, R("landd", t * CH + c0, t * CH + c1), cn)
+            tt(R("mq", c0, c1), m, R("maskc", c0, c1), ALU.add)
+            m2c = t * CH + c0
+            tt(R("m2", m2c, m2c + nc), R("mq", c0, c1), w, ALU.mult)
+            if t < RO - 1 or s < NS - 1:
+                of = R("offf", k0, k0 + K)
+                if CFG["tomb_s"]:
+                    for k in range(K):
+                        act(R("junk", c0 + 16 * k, c0 + 16 * k + 16), R("m2", m2c + 16 * k, m2c + 16 * k + 16), ACT.Identity, scale=-1.0,
+                            bias=R("bc", k0 + k, k0 + k + 1), accum_out=R("offf", k0 + k, k0 + k + 1))
+                else:
+                    vec("tensor_tensor_scan", R("hold2", c0, c1), R("nmask", 0, nc), R("m2", m2c, m2c + nc), 0.0, ALU.mult, ALU.add)
+                    tt(of, R("bc", k0, k0 + K), R("hold2", c0 + 15, c1, 16), ALU.subtract)
+                ot = R("offt", 8 * s, 8 * s + K)
+                vec("tensor_copy", ot, of)
+                vec("tensor_copy", IND(xwin, ot), R("c512", 0, nc))
+    yb = CFG["banks"][0][2][0]
+    for t in range(RO):
+        o = R(yb, t * CH, (t + 1) * CH, 1, 0, 8)
+        mms([(o, R("g8"), R("maskd")), (o, R("g8n"), R("m2", t * CH, (t + 1) * CH))])
+    ts(R("yts", 0, RO * CH, 1, 0, 8), R(yb, 0, RO * CH, 1, 0, 8), float(V), ALU.min)
+    dma("s", ("d", "yt", None), R("yts", 0, RO * CH, 1, 0, 8), 8 * RO * CH * 4)
+    return ops
+
+
+MODELS = [
+    {"f": 1.05, "g": 1.15, "sc": 2.0, "pe": 0.44, "pm": 0, "hx": 70, "hs": 50, "ri": 400, "rl": 1800, "bw": 350.0},
+    {"f": 1.25, "g": 1.56, "sc": 3.8, "pe": 0.52, "pm": 0, "hx": 100, "hs": 70, "ri": 700, "rl": 2500, "bw": 250.0},
+    {"f": 1.4, "g": 2.0, "sc": 5.5, "pe": 0.6, "pm": 0, "hx": 130, "hs": 90, "ri": 1000, "rl": 3200, "bw": 180.0},
+]
+UNIT = [55.0, 70.0, 90.0]
+ENG = {"v": 0, "s": 1, "t": 2, "g": 3, "y": 4, None: 5}
+
+
+def times(op, m):
+    c = op["cost"]
+    k = c[0]
+    if k in ("v", "s"):
+        d = max(64, c[1]) * 0.83 * m["f"]
+    elif k == "g":
+        d = (55 + c[1] * m["g"] * 0.83) * m["f"]
+    elif k == "sc":
+        d = (50 + c[1] * m["sc"] * 0.83) * m["f"]
+    elif k == "t":
+        d = c[1] * m["pe"] + 30 + c[2] * m["pm"]
+    elif k == "io":
+        d = (130 + 2 * c[1] * 0.83) * m["f"]
+    elif k == "dma":
+        return 60, 1600
+    elif k == "r":
+        return m["ri"], m["ri"]
+    else:
+        return 0, m["rl"] - m["ri"]
+    return d, d
+
+
+def table(ops, m):
+    tb = []
+    for op in ops:
+        e, dl = op["eng"], []
+        for o, k in op["deps"].items():
+            p = ops[o]
+            if k == "ord":
+                if e is None:
+                    dl.append((o, 0))
+            elif p["eng"] != e or p["kind"] != "c" or op["kind"] != "c":
+                dl.append((o, m["hx"]))
+            else:
+                dl.append((o, m["hs"]))
+        hold, lat = times(op, m)
+        tb.append((ENG[e], hold, lat, op["cost"][1] / m["bw"] if op["kind"] == "dma" else -1, dl, [int(b[2]) for b in op["banks"]]))
+    return tb, m["hx"]
+
+
+def fresh(n):
+    return [[0.0] * 6, [0.0] * n, [[-1e9] * 3 for b in range(8)], [0.0]]
+
+
+def place(tab, i, st):
+    tb, hx = tab
+    e, hold, lat, dm, dl, bk = tb[i]
+    s, fin = st[0][e], st[1]
+    for o, d in dl:
+        if fin[o] + d > s:
+            s = fin[o] + d
+    for b in bk:
+        x = st[2][b]
+        for e2 in (0, 1, 2):
+            if e2 != e and x[e2] + hx > s:
+                s = x[e2] + hx
+    return s
+
+
+def commit(tab, i, st, s):
+    e, hold, lat, dm, dl, bk = tab[0][i]
+    f = s + lat
+    if dm >= 0:
+        f = st[3][0] = max(f, st[3][0]) + dm
+    st[1][i] = f
+    if e < 5:
+        st[0][e] = s + hold
+    for b in bk:
+        st[2][b][e] = f
+
+
+def replay(tab, order):
+    st = fresh(len(order))
+    for i in order:
+        commit(tab, i, st, place(tab, i, st))
+    return max(st[1]) + 0.05 * sum(st[1]) / len(order)
+
+
+def schedule(ops):
+    n = len(ops)
+    succ = [[] for i in range(n)]
+    for i, op in enumerate(ops):
+        for o in op["deps"]:
+            succ[o].append(i)
+    tabs = [table(ops, m) for m in MODELS]
+    tab = tabs[1]
+    lev = [0.0] * n
+    for i in range(n - 1, -1, -1):
+        lev[i] = tab[0][i][2] + max(tab[0][i][3], 0) + max([lev[j] + tab[1] for j in succ[i]], default=0.0)
+    x = [CFG["seed"]]
+
+    def rnd():
+        x[0] = (x[0] * 1103515245 + 12345) % 2147483648
+        return x[0] / 2147483648.0
+
+    def decode(pr, win):
+        st = fresh(n)
+        left = [len(op["deps"]) for op in ops]
+        ready = [i for i in range(n) if left[i] == 0]
+        order = []
+        while ready:
+            ss = [(place(tab, i, st), i) for i in ready]
+            s0, i0 = min(ss)
+            e0 = tab[0][i0][0]
+            s, i = max([c for c in ss if c[0] <= s0 + win and tab[0][c[1]][0] == e0], key=lambda c: pr[c[1]] - 2 * (c[0] - s0))
+            commit(tab, i, st, s)
+            order.append(i)
+            ready.remove(i)
+            for j in succ[i]:
+                left[j] -= 1
+                if left[j] == 0:
+                    ready.append(j)
+        return order
+    best = None
+    for it in range(CFG["tries"]):
+        jit = 1500 * rnd() ** 2
+        order = decode([v + jit * rnd() + op["bias"] for v, op in zip(lev, ops)], 1000 * rnd())
+        sc = [replay(tb, order) for tb in tabs]
+        v = sum(a / b for a, b in zip(sc, UNIT))
+        if best is None or v < best[0]:
+            best = (v, order, sc)
+    return best
+
+
+def plan():
+    ops = build()
+    v, order, sc = schedule(ops)
+    place_of = {o: k for k, o in enumerate(order)}
+    pos, cnt = {}, {}
+    known = {e: {} for e in "vstgy"}
+    clock, bank, waits, need = {}, {}, {}, set()
+    for i in order:
+        op = ops[i]
+        e = op["eng"]
+        if e is None:
+            clock[i] = {("x", i): 1}
+            continue
+        want = {o for o, k in op["deps"].items() if k != "ord"}
+        for b in op["banks"]:
+            for e2, o in bank.get(b, {}).items():
+                if e2 != e:
+                    want.add(o)
+            bank.setdefault(b, {})[e] = i
+        kn, ws = known[e], []
+        for o in sorted(want, key=lambda o: -place_of[o]):
+            key, val = pos[o] if o in pos else (("x", o), 1)
+            if kn.get(key, 0) < val:
+                ws.append(o)
+                need.add(o)
+                for k2, v2 in clock[o].items():
+                    if kn.get(k2, 0) < v2:
+                        kn[k2] = v2
+        waits[i] = ws
+        clock[i] = dict(kn)
+        if op["kind"] == "c":
+            cnt[e] = cnt.get(e, 0) + 1
+            pos[i] = (e, cnt[e])
+            clock[i][e] = cnt[e]
+        else:
+            clock[i][("x", i)] = 1
+    return ops, order, waits, need, sc
+
+
+PLAN = []
+
+
+def rank_program(g, core, T, topo):
+    rank = T.rank_of(core)
+    if rank is None:
+        return
+    if not PLAN:
+        PLAN.append(plan())
+    ops, order, waits, need, sc = PLAN[0]
+    dst = [T.cores[(rank + 1 + t % (N - 1)) % N] for t in range(RO)]
+    src = [T.cores[(rank - 1 - t % (N - 1)) % N] for t in range(RO)]
+
+    def lanes(a):
+        r = T.rank_of(a)
+        m = -1
+        for t in range(RO):
+            m &= topo.mask(a, T.cores[(r + 1 + t % (N - 1)) % N])
+        return m
+    Q = {"v": g.vector, "s": g.scalar, "t": g.tensor, "g": g, "y": g.sync}
+
+    def A(a):
+        if not isref(a):
+            return a
+        if a[0] == "i":
+            return A(a[1]).indirect(A(a[2]))
+        if a[0] == "d":
+            return T[a[1]][:] if a[2] is None else T[a[1]][:, a[2][0]:a[2][1]]
+        if a[6] == 1:
+            return T[a[1]][a[2]:a[3], a[4]:a[5]]
+        return T[a[1]][a[2]:a[3], a[4]:a[5]:a[6]]
+    at, cnt, sent, last = {}, {}, 0, []
+    for i in order:
+        op = ops[i]
+        e = op["eng"]
+        if e is None:
+            at[i] = (op["x"][1], bin(lanes(src[op["x"][0]])).count("1"))
+            continue
+        q = Q[e]
+        for o in waits[i]:
+            q.wait_ge(T.sem[at[o][0]], at[o][1])
+        if op["kind"] == "rdma":
+            t, sem = op["x"]
+            rid, pid = topo.addr(dst[t])[:2]
+            a = op["ins"][0][1]
+            g.remote_dma(A(a[0]), A(a[1]), T.sem[sem], T.sem["sent"], pid, rid, lanes(core))
+            sent += bin(lanes(core)).count("1")
+            continue
+        for m, args, kw in op["ins"]:
+            ins = CALL[m](q, [A(x) for x in args], {n: A(x) for n, x in kw.items()})
+        if op["kind"] == "dma":
+            ins.then_inc(T.sem[op["x"]], 16)
+            at[i] = (op["x"], 16)
+            if i not in need:
+                last.append((q, op["x"]))
+        elif i in need:
+            cnt[e] = cnt.get(e, 0) + 1
+            ins.then_inc(T.sem["q" + e], 1)
+            at[i] = ("q" + e, cnt[e])
+    g.wait_ge(T.sem["sent"], sent)
+    for q, sem in last:
+        q.wait_ge(T.sem[sem], 16)
+
+
+CALL = {
+    "matmul": lambda q, a, k: q.matmul(*a),
+    "activation": lambda q, a, k: q.activation(*a, **k),
+    "tensor_copy": lambda q, a, k: q.tensor_copy(*a),
+    "tensor_tensor": lambda q, a, k: q.tensor_tensor(*a),
+    "tensor_scalar": lambda q, a, k: q.tensor_scalar(*a),
+    "tensor_tensor_scan": lambda q, a, k: q.tensor_tensor_scan(*a),
+    "memset": lambda q, a, k: q.memset(*a),
+    "iota": lambda q, a, k: q.iota(*a, **k),
+    "dma_start": lambda q, a, k: q.dma_start(*a),
+}

@@ -1,23 +1,24 @@
+import math
 from concourse.mybir import AluOpType as ALU, ActivationFunctionType as ACT
 
 V, HB, CH, RO, N = 2048, 4096, 96, 3, 8
 XW = V + 112
+A_, P_ = "abs", "pe"
 CFG = {
     "streams": [(0, 48), (48, 96)],
-    "banks": [(("ps0", 0), ("ps1", 0), ["ps4", "ps5"]), (("ps2", 0), ("ps3", 0), ["ps6", "ps7"])],
-    "le": [[['sv', 'sv', 'vs'], ['vv', 'vs', 's']], [['sv', 'vs', 's'], ['vs', 'vs', 'vs']], [['vs', 's', 'sv'], ['sv', 'vs', 'vs']]],
-    "xe": [[['sv', 'vs', 'vv'], ['sv', 'vv', 'vv']], [['vs', 'vv', 'vv'], ['sv', 'vs', 'vv']], [['vv', 'sv', 'vv'], ['sv', 'sv', 'vv']]],
-    "how": [[['pe', 'pe', 'abs'], ['pe', 'pe', 'abs']], [['pe', 'pe', 'abs'], ['pe', 'pe', 'abs']], [['abs', 'pe', 'abs'], ['pe', 'pe', 'abs']]],
-    "bias": [[-2000, -2000], [1000, 0], [1000, 0]],
-    "split": True,
-    "tomb_s": True,
-    "xfirst": False,
-    "seed": 595, "tries": 4,
+    "banks": [("ps0", "ps1", ["ps4", "ps5"]), ("ps2", "ps3", ["ps6", "ps7"])],
+    "lp": [[[[24, 24]] * 3] * 2] * 3,
+    "xp": [[[[(24, P_), (24, P_)]] * 3] * 2] * 3,
+    "early": [[0, 0]] * 3, "pre": 1, "sign": 0, "sq": 0, "sint": 0, "gd": 0, "join": 0, "split": [1, 1],
+    "sx": [[[1, 1, 1]] * 2] * 3,
+    "msum": [[0, 0]] * 3,
+    "dead": [20000, 26500, 33000, 39500, 46000, 52500],
+    "win": 300, "seed": 2, "steps": 55000, "heat": 20.0, "pull": [0.3, 0.3, 0.3, 0.2, 0.1, 0.0], "models": [1, 3],
 }
-MAXS = 2
+MAXS = 3
 
 SCRATCH = {
-    "hdw": ("sbuf", [128, HB], "int32"), "nxw": ("sbuf", [128, V + 8], "int32"),
+    "hdw": ("sbuf", [128, HB + 8], "int32"), "nxw": ("sbuf", [128, V + 8], "int32"),
     "xw": ("sbuf", [128, XW], "bfloat16"),
     "c0b": ("sbuf", [128, CH], "bfloat16"), "wtb": ("sbuf", [128, 16], "bfloat16"),
     "thi": ("sbuf", [128, 4], "int32"), "thf": ("sbuf", [128, 4], "float32"),
@@ -28,34 +29,32 @@ SCRATCH = {
     "tmpd": ("sbuf", [128, 128], "float32"),
     "rot": ("sbuf", [128, 128], "bfloat16"), "rott": ("sbuf", [128, 128], "bfloat16"), "wsh": ("sbuf", [128, 128], "bfloat16"),
     "idb": ("sbuf", [128, 128], "bfloat16"), "nidb": ("sbuf", [128, 128], "bfloat16"),
-    "idh": ("sbuf", [128, 128], "float16"), "nidh": ("sbuf", [128, 128], "float16"),
-    "oneh": ("sbuf", [128, 128], "float16"), "kblk": ("sbuf", [128, 128], "bfloat16"),
-    "trih": ("sbuf", [128, 128], "float16"), "o4h": ("sbuf", [128, 128], "float16"),
+    "idh": ("sbuf", [128, 128], "float16"), "nidh": ("sbuf", [128, 128], "float16"), "n4h": ("sbuf", [128, 128], "float16"),
+    "oneh": ("sbuf", [128, 128], "float16"), "trih": ("sbuf", [128, 128], "float16"),
+    "o4h": ("sbuf", [128, 128], "float16"), "o4n": ("sbuf", [128, 128], "float16"),
+    "base": ("sbuf", [128, 2 * CH], "bfloat16"), "zero": ("sbuf", [128, 2 * CH], "bfloat16"),
     "ed": ("sbuf", [128, 2048], "float16"),
     "b1": ("sbuf", [128, 144], "bfloat16"), "b2": ("sbuf", [128, 144], "bfloat16"), "bn": ("sbuf", [128, 144], "bfloat16"),
     "rio": ("sbuf", [128, 1024], "bfloat16"), "rr": ("sbuf", [128, 1024], "bfloat16"),
-    "nmask": ("sbuf", [128, CH], "float32"), "maskc": ("sbuf", [128, CH], "float32"), "maskd": ("sbuf", [128, CH], "float32"),
-    "placec": ("sbuf", [128, CH], "float32"), "placed": ("sbuf", [128, CH], "float32"),
-    "bc": ("sbuf", [128, 8], "float32"),
-    "g8": ("sbuf", [128, 8], "float32"), "g8n": ("sbuf", [128, 8], "float32"),
+    "nmask": ("sbuf", [128, CH], "float32"), "maskd": ("sbuf", [128, CH], "float32"),
+    "placed": ("sbuf", [128, CH], "float32"), "ct": ("sbuf", [128, CH], "float16"),
+    "g8a": ("sbuf", [128, 8], "float16"), "g8b": ("sbuf", [128, 8], "float16"),
     "c512": ("sbuf", [128, CH], "bfloat16"),
     "landd": ("sbuf", [128, 2 * CH], "bfloat16"), "lande": ("sbuf", [128, 2 * CH], "bfloat16"), "landf": ("sbuf", [128, CH], "float32"),
     "dsb": ("sbuf", [128, RO * CH], "bfloat16"), "dtb": ("sbuf", [128, 128 * MAXS], "bfloat16"),
     "h1": ("sbuf", [128, CH], "int32"), "h2": ("sbuf", [128, CH], "int32"), "h3": ("sbuf", [128, CH], "int32"),
     "h4": ("sbuf", [128, CH], "int32"), "h5": ("sbuf", [128, CH], "int32"), "hu": ("sbuf", [128, CH], "uint16"),
-    "off": ("sbuf", [128, 3 * CH], "uint16"), "cand": ("sbuf", [128, 3 * CH], "float16"),
+    "off": ("sbuf", [128, 3 * CH], "uint16"), "sl": ("sbuf", [128, 48 * CH], "float16"),
+    "cx": ("sbuf", [128, 1024], "float16"), "drep3": ("sbuf", [128, CH, 16], "bfloat16"),
     "gl0": ("sbuf", [128, 16 * CH], "float16"), "gl1": ("sbuf", [128, 16 * CH], "float16"), "gl2": ("sbuf", [128, 16 * CH], "float16"),
-    "gx0": ("sbuf", [128, 16 * CH], "bfloat16"), "gx1": ("sbuf", [128, 16 * CH], "bfloat16"), "gx2": ("sbuf", [128, 16 * CH], "bfloat16"),
-    "zz0": ("sbuf", [128, 16 * CH], "bfloat16"), "zz1": ("sbuf", [128, 16 * CH], "bfloat16"), "zz2": ("sbuf", [128, 16 * CH], "bfloat16"),
+    "gx": ("sbuf", [128, 48 * CH], "bfloat16"), "zz": ("sbuf", [128, 48 * CH], "bfloat16"),
     "drep": ("sbuf", [128, 16 * CH], "bfloat16"),
     "near": ("sbuf", [128, 3 * CH], "float16"), "yy": ("sbuf", [128, 3 * CH], "float16"),
-    "mm": ("sbuf", [128, CH], "float32"), "hold": ("sbuf", [128, CH], "float32"), "mq": ("sbuf", [128, CH], "float32"),
-    "hold2": ("sbuf", [128, CH], "float32"),
-    "m2": ("sbuf", [128, RO * CH], "float32"), "offw": ("sbuf", [128, 8 * MAXS], "uint16"), "offt": ("sbuf", [128, 8 * MAXS], "uint16"),
-    "offf": ("sbuf", [128, 8], "float32"), "junk": ("sbuf", [128, CH], "float32"),
-    "ee": ("sbuf", [128, 4 * CH], "bfloat16"), "zs": ("sbuf", [128, CH], "bfloat16"), "dl": ("sbuf", [128, CH], "int32"),
-    "ww": ("sbuf", [128, CH], "bfloat16"), "dw": ("sbuf", [128, RO * CH], "bfloat16"), "cn": ("sbuf", [128, 2 * CH], "bfloat16"),
-    "cf": ("sbuf", [128, CH], "float32"), "yts": ("sbuf", [128, RO * CH], "float32"),
+    "mm": ("sbuf", [128, RO * CH], "float16"), "hold": ("sbuf", [128, 128 * MAXS], "float32"), "hold2": ("sbuf", [128, CH], "float32"),
+    "offw": ("sbuf", [128, 8 * MAXS], "uint16"), "offt": ("sbuf", [128, 8 * MAXS], "uint16"),
+    "ee": ("sbuf", [128, 4 * CH], "float16"), "zs": ("sbuf", [128, CH], "float16"), "dl": ("sbuf", [128, CH], "int32"),
+    "ww": ("sbuf", [128, RO * CH], "float16"), "dw": ("sbuf", [128, RO * CH], "bfloat16"),
+    "cn": ("sbuf", [128, 2 * CH], "bfloat16"), "cf": ("sbuf", [128, CH], "float32"), "yts": ("sbuf", [128, RO * CH], "float32"),
 }
 for b in range(8):
     SCRATCH["ps%d" % b] = ("psum", [128, 512], "float32")
@@ -74,42 +73,49 @@ def IND(win, off):
 
 
 def isref(a):
-    return isinstance(a, tuple) and len(a) > 0 and a[0] in ("r", "i", "d")
+    return isinstance(a, tuple) and len(a) > 0 and a[0] in ("r", "i", "d", "3")
 
 
 def cols(r):
     if r[0] == "i":
         return 16 * cols(r[2])
+    if r[0] == "3":
+        return (r[5] - r[4]) // 16 * (r[8] - r[7])
     return len(range(r[4], r[5], r[6]))
 
 
 def width(r):
-    return BYTES[SCRATCH[(r[1] if r[0] == "r" else r[1][1])][2]]
+    return BYTES[SCRATCH[(r[1] if r[0] != "i" else r[1][1])][2]]
 
 
 def build():
-    ops, log, tag = [], {}, [0]
+    ops, log, tag, run = [], {}, ["-"], [0]
+
+    def together(on=True):
+        run[0] = int(on)
     STREAMS = CFG["streams"]
     NS = len(STREAMS)
 
-    def add(eng, ins, cost, kind="c", after=(), extra=None):
+    def add(eng, ins, cost, kind="c", after=(), extra=None, alt=None):
         rd, wr = [], []
         for m, args, kw in ins:
-            refs = [(i == 0, a) for i, a in enumerate(args) if isref(a)] + [(k == "accum_out", a) for k, a in kw.items() if isref(a)]
+            refs = [(i == 0, a) for i, a in enumerate(args) if isref(a)] + [(False, a) for a in kw.values() if isref(a)]
             for out, a in refs:
                 if kind == "rdma" and out:
                     continue
                 if a[0] == "i":
                     rd.append(a[2])
                     (wr if out else rd).append(a[1])
-                elif a[0] == "r":
+                elif a[0] != "d":
                     (wr if out else rd).append(a)
-        me = len(ops)
+        join = run[0] > 1 and CFG["join"]
+        run[0] += run[0] > 0
+        me = len(ops) - join
         deps = {}
         for isw, lst in ((False, rd), (True, wr)):
             for a in lst:
                 for o, ow, b in log.get(a[1], []):
-                    if (isw or ow) and a[2] < b[3] and b[2] < a[3] and a[4] < b[5] and b[4] < a[5]:
+                    if (isw or ow) and a[2] < b[3] and b[2] < a[3] and a[4] < b[5] and b[4] < a[5] and (a[0] != "3" or (a[7] < b[8] and b[7] < a[8])):
                         deps[o] = "ord" if (eng == "t" and ops[o]["eng"] == "t") else "raw"
         for o in after:
             deps.setdefault(o, "ord")
@@ -119,42 +125,66 @@ def build():
                     log[a[1]] = [x for x in log.get(a[1], []) if not (a[2] <= x[2][2] and x[2][3] <= a[3] and a[4] <= x[2][4] and x[2][5] <= a[5])]
                 log.setdefault(a[1], []).append((me, isw, a))
         banks = sorted({a[1] for a in rd + wr if a[1].startswith("ps")})
-        ops.append({"bias": tag[0], "eng": eng, "ins": ins, "cost": cost, "kind": kind, "deps": deps, "banks": banks, "x": extra})
+        forms = {eng: (ins, cost)}
+        if alt:
+            forms["s"] = alt
+        if join:
+            op = ops[me]
+            wait = [("wait", (), {})] if deps.pop(me, None) else []
+            op["forms"] = {e: (i0 + wait + forms[e][0], ("run", c0, forms[e][1], len(wait))) for e, (i0, c0) in op["forms"].items() if e in forms}
+            op["ins"], op["cost"] = op["forms"][eng]
+            op["deps"].update(deps)
+            op["banks"] = sorted(set(op["banks"] + banks))
+            return me
+        ops.append({"ph": tag[0], "eng": eng, "ins": ins, "cost": cost, "kind": kind, "deps": deps, "banks": banks, "x": extra, "forms": forms})
         return me
 
-    def vec(m, *args, **kw):
+    def vec(m, *args, alt=None):
         refs = [a for a in args if isref(a)]
         n = cols(args[0])
         if args[0][0] == "i":
             cost = ("sc", n)
         elif any(a[0] == "i" for a in refs):
-            cost = ("g", n)
+            cost = ("gt" if m == "tensor_tensor" else "g", n)
         else:
             big = [a for a in refs if cols(a) == n]
             f = 0.5 if all(width(a) == 2 for a in big) else 1.0
             if m == "tensor_tensor":
                 f = 1.0 if any(a[1].startswith("ps") for a in big[1:]) else 2.0
             cost = ("v", n * f)
-        return add("v", [(m, args, kw)], cost)
+        return add("v", [(m, args, {})], cost, alt=alt)
 
-    def ts(out, a, s1, op0, s2=None, op1=None):
-        return vec("tensor_scalar", out, a, s1, s2, op0) if op1 is None else vec("tensor_scalar", out, a, s1, s2, op0, op1)
+    def ts(out, a, s1, op0, s2=None, op1=None, alt=None):
+        if tag[0] == "-" and op0 == ALU.mult and op1 in (None, ALU.add):
+            alt = actf(out, a, ACT.Identity, scale=s1, bias=0.0 if op1 is None else s2)
+        return vec("tensor_scalar", out, a, s1, s2, op0, alt=alt) if op1 is None else vec("tensor_scalar", out, a, s1, s2, op0, op1, alt=alt)
 
     def tt(out, a, b, op):
         return vec("tensor_tensor", out, a, b, op)
 
+    def actf(out, a, f, **kw):
+        return [("activation", (out, a, f), kw)], ("gs" if a[0] == "i" else "s", cols(a))
+
     def act(out, a, f, **kw):
-        return add("s", [("activation", (out, a, f), kw)], ("g" if a[0] == "i" else "s", cols(a)))
+        return add("s", *actf(out, a, f, **kw))
 
-    def copy(e, out, a):
-        return vec("tensor_copy", out, a) if e == "v" else act(out, a, ACT.Copy)
+    def copy(out, a):
+        return vec("tensor_copy", out, a, alt=actf(out, a, ACT.Copy))
 
-    def mms(lst):
+    inbank, shut = {}, {}
+
+    def mms(lst, start=True, stop=True):
         ins, c = [], 0
         for i, (o, l, r) in enumerate(lst):
-            ins.append(("matmul", (o, l, r, i == 0, i == len(lst) - 1), {}))
+            ins.append(("matmul", (o, l, r, start and i == 0, stop and i == len(lst) - 1), {}))
             c += max(min(64, cols(l)), cols(r)) * (4 if width(l) == 4 else 1)
-        return add("t", ins, ("t", c, len(lst)))
+        bank = lst[0][0][1]
+        after = list(inbank.get(bank, [])) if start != stop else [shut[bank]] if bank in shut else []
+        me = add("t", ins, ("t", c, len(lst)), after=after)
+        if start != stop:
+            inbank[bank], shut[bank] = [], me
+        inbank.setdefault(bank, []).append(me)
+        return me
 
     nd = [0]
 
@@ -170,343 +200,539 @@ def build():
         o = add("g", [("remote", (dst, src), {})], ("r",), "rdma", (), (t, sem))
         return add(None, [("arrive", (dst,), {})], ("a",), "arr", (o,), (t, sem))
 
+    turn = 8 if CFG["sq"] else 0
     a = dma("y", R("c0b"), ("d", "c0", None), 24576)
-    a = dma("y", R("hdw"), ("d", "hd", None), 128 * HB * 4, (a,))
-    rest = [(R("nxw", 0, V), ("d", "nx", None), 128 * V * 4), (R("xw", 0, V), ("d", "xr", None), 128 * V * 2)]
-    if CFG["xfirst"]:
-        rest.reverse()
-    for o, i, n in rest:
+    a = dma("y", R("hdw", turn, HB + turn), ("d", "hd", None), 128 * HB * 4, (a,))
+    for o, i, n in [(R("nxw", 0, V), ("d", "nx", None), 128 * V * 4), (R("xw", 0, V), ("d", "xr", None), 128 * V * 2)]:
         a = dma("y", o, i, n, (a,))
     a = dma("s", R("wtb"), ("d", "wt", None), 4096)
+    if turn:
+        a = dma("s", R("hdw", 0, turn), ("d", "hd", (HB - turn, HB)), 4096, (a,))
     a = dma("s", R("thi", 0, 1), ("d", "th", None), 512, (a,))
     W = 16 * max(b - a for a, b in STREAMS)
-    hows = {x for a in CFG["how"] for b in a for x in b}
+    hows = {x[1] for a in CFG["xp"] for b in a for c in b for x in c}
     imp = {"allow_small_or_imprecise_dtypes": True}
     add("g", [("iota", (R("pi", 0, 1), [[0, 1]], 0, 1), {})], ("io", 1))
     add("g", [("iota", (R("gcol"), [[1, 8], [0, 16]], 0, 0), imp)], ("io", 128))
     add("g", [("iota", (R("dcol"), [[0, 8], [1, 16]], 0, 0), imp)], ("io", 128))
     add("g", [("iota", (R("rio", 0, W), [[1, W // 16], [0, 16]], 0, -1), imp)], ("io", W))
+    together()
     ts(R("pi", 1, 2), R("pi", 0, 1), 4, ALU.arith_shift_right)
     ts(R("pi", 2, 3), R("pi", 0, 1), 15, ALU.bitwise_and)
     vec("tensor_copy", R("pf", 1, 3), R("pi", 1, 3))
     pg, pd = R("pf", 1, 2), R("pf", 2, 3)
+    together()
     ts(R("blk"), R("gcol"), pg, ALU.is_equal)
     ts(R("deq"), R("dcol"), pd, ALU.is_equal)
-    vec("tensor_copy", R("tmpa", 0, 127), R("deq", 1, 128))
-    vec("tensor_copy", R("tmpa", 127, 128), R("deq", 0, 1))
-    tt(R("rot"), R("tmpa"), R("blk"), ALU.mult)
-    vec("tensor_copy", R("tmpc", 1, 128), R("deq", 0, 127))
-    vec("tensor_copy", R("tmpc", 0, 1), R("deq", 127, 128))
+    copy(R("tmpc", 1, 128), R("deq", 0, 127))
+    copy(R("tmpc", 0, 1), R("deq", 127, 128))
     tt(R("rott"), R("tmpc"), R("blk"), ALU.mult)
+    together()
+    copy(R("tmpa", 0, 127), R("deq", 1, 128))
+    copy(R("tmpa", 127, 128), R("deq", 0, 1))
+    tt(R("rot"), R("tmpa"), R("blk"), ALU.mult)
+    together(False)
     mms([(R("ps7", 0, 16), R("rott"), R("wtb"))])
+    together()
     for gq in range(8):
         ts(R("wsh", 16 * gq, 16 * gq + 16), R("ps7", 0, 16), R("blk", 16 * gq, 16 * gq + 1), ALU.mult)
+    together()
     tt(R("idh"), R("deq"), R("blk"), ALU.mult)
-    for d in range(16):
-        ts(R("ed", 128 * d, 128 * d + 128), R("idh"), R("deq", d, d + 1), ALU.mult)
-    ts(R("nidb"), R("idh"), -1.0, ALU.mult)
     ts(R("nidh"), R("idh"), -1.0, ALU.mult)
-    vec("tensor_copy", R("idb"), R("idh"))
-    vec("tensor_copy", R("oneh"), R("blk"))
-    ts(R("kblk"), R("oneh"), 1024.0, ALU.mult)
+    for d in range(16 if any(x == 0 for a in CFG["sx"] for b in a for x in b) else 0):
+        if d % 4 == 0:
+            together()
+        ts(R("ed", 128 * d, 128 * d + 128), R("nidh"), R("deq", d, d + 1), ALU.mult)
+    together(False)
+    ts(R("nidb"), R("idh"), -1.0, ALU.mult)
+    if CFG["sign"]:
+        copy(R("idb"), R("idh"))
+    together()
+    copy(R("oneh"), R("blk"))
     ts(R("o4h"), R("oneh"), -4096.0, ALU.mult)
+    together()
     ts(R("tmpb"), R("dcol"), pd, ALU.is_gt)
     tt(R("tmpd"), R("tmpb"), R("deq"), ALU.subtract)
-    tt(R("trih"), R("tmpd"), R("o4h"), ALU.mult)
+    together(False)
+    if CFG["sign"]:
+        ts(R("o4n"), R("oneh"), -2048.0, ALU.mult)
+        for l in range(3):
+            ts(R("pf", 4 + l, 5 + l), pd, 16.0 * l, ALU.add, -2048.0, ALU.mult)
+            ts(R("base", l * W // 16, (l + 1) * W // 16), R("deq", 0, W // 16), 0.0, ALU.mult, R("pf", 4 + l, 5 + l), ALU.add)
+    o4n = R("o4n" if CFG["sign"] else "o4h")
+    tt(R("trih"), R("tmpd"), o4n, ALU.mult)
     bs = [("b1", 1.0)] if hows & {"pe", "abs"} else []
     if "relu" in hows:
         bs += [("b2", 2.0), ("bn", -1.0)]
     for nm, f in bs:
+        together()
         vec("memset", R(nm), 0.0)
         ts(R(nm, 15, 128, 16), R("blk", 0, 128, 16), f, ALU.mult)
+    together(False)
     ts(R("rr", 0, W), R("rio", 0, W), 0.0, ALU.is_equal)
+    together()
+    if any(x for a in CFG["sx"] for b in a for x in b):
+        ts(R("tmpa"), R("dcol"), pd, ALU.is_lt, -6144.0, ALU.mult)
+        ts(R("tmpc"), R("deq"), 4096.0, ALU.mult)
+        tt(R("cx", 0, 128), R("tmpa"), R("tmpc"), ALU.add)
+        ts(R("cx", 15, 128, 16), R("cx", 15, 128, 16), -6144.0, ALU.add)
+        for n in (128, 256, 512):
+            vec("tensor_copy", R("cx", n, 2 * n), R("cx", 0, n))
     mask = "deq"
+    together()
     ts(R("nmask"), R(mask, 0, CH), -1.0, ALU.mult, 1.0, ALU.add)
-    ts(R("pf", 3, 4), pd, 1.0, ALU.add)
-    ts(R("placec"), R("gcol", 0, CH), 16.0, ALU.mult, R("pf", 3, 4), ALU.add)
-    ts(R("placed"), R("placec"), float(V), ALU.add)
-    ts(R("bc", 0, 6), R("placed", 0, CH, 16), 0.0625 if CFG["tomb_s"] else 1.0, ALU.mult)
-    tt(R("maskc"), R("placec"), R(mask, 0, CH), ALU.mult)
+    ts(R("g8a"), R("blk", 0, 128, 16), -1.0, ALU.mult)
+    ts(R("g8b"), R("blk", 0, 128, 16), -256.0, ALU.mult)
+    ts(R("ct"), R("nmask"), 4096.0, ALU.mult, float(V), ALU.add)
+    together()
+    ts(R("pf", 3, 4), pd, -1.0, ALU.mult, -float(V + 1), ALU.add)
+    ts(R("placed"), R("gcol", 0, CH), -16.0, ALU.mult, R("pf", 3, 4), ALU.add)
     tt(R("maskd"), R("placed"), R(mask, 0, CH), ALU.mult)
-    vec("tensor_copy", R("g8"), R("blk", 0, 128, 16))
-    ts(R("g8n"), R("g8"), -1.0, ALU.mult)
+    together()
+    vec("memset", R("hold"), 0.0)
     vec("memset", R("c512"), 512.0)
     vec("memset", R("xw", V, XW), 512.0)
     vec("memset", R("nxw", V, V + 8), V)
+    together(False)
     vec("tensor_copy", R("thf", 0, 1), R("thi", 0, 1))
+    if CFG["sign"]:
+        ts(R("thf", 1, 2), R("thf", 0, 1), 0.5, ALU.add)
+    if CFG["sq"]:
+        vec("memset", R("thf", 2, 3), 16.0)
 
     xwin = R("xw")
     for t in range(RO):
         for s, (c0, c1) in enumerate(STREAMS):
             nc = c1 - c0
-            tag[0] = CFG["bias"][t][s]
-            (Pb, p0), (Qb, q0), zb = CFG["banks"][s]
+            tag[0] = NS * t + s
+            Pb, Qb, zb = CFG["banks"][s]
             NZ = len(zb)
-            src = [R("c0b", c0, c1)] if t == 0 else [R("landd", (t - 1) * CH + c0, (t - 1) * CH + c1)]
-            if t > 0 and CFG["split"]:
-                src.append(R("lande", (t - 1) * CH + c0, (t - 1) * CH + c1))
+            src = [R("c0b", c0, c1)] if t == 0 else [R(n, (t - 1) * CH + c0, (t - 1) * CH + c1) for n in ("landd", "lande")[1 - CFG["split"][t - 1]:]]
             D = R("dsb", t * CH + c0, t * CH + c1)
             DT = R("dtb", 128 * s, 128 * s + 128, 1, 0, nc)
-            ph = R(Pb, p0, p0 + nc)
+            ph = R(Pb, 0, nc)
             mms([(ph, R("wsh"), x) for x in src])
-            pD, pDT = R(Qb, q0, q0 + nc), R(Qb, q0 + 3 * nc, q0 + 3 * nc + 128, 1, 0, nc)
-            mms([(pDT, x, R("rot")) for x in src])
+            pD, pDT = R(Qb, 0, nc), R(Qb, 3 * nc, 3 * nc + 128, 1, 0, nc)
+            if not CFG["gd"] or any(h == "pe" for p in CFG["xp"][t][s] for n, h in p):
+                mms([(pDT, x, R("rot")) for x in src])
+                copy(DT, pDT)
             mms([(pD, R("rot"), x) for x in src])
-            act(DT, pDT, ACT.Copy)
-            act(D, pD, ACT.Copy)
-            if CFG["split"] and t < RO - 1:
+            copy(D, pD)
+            if t < RO - 1 and CFG["split"][t]:
                 send(t, R("landd", t * CH + c0, t * CH + c1), D)
             h = [R("h%d" % i, c0, c1) for i in range(1, 6)]
             vec("tensor_copy", h[0], ph)
+            together()
             ts(h[1], h[0], HB - 1, ALU.bitwise_and)
             ts(h[2], h[1], 32.0, ALU.add)
             tt(h[3], h[1], h[2], ALU.mult)
             ts(h[4], h[3], 5, ALU.arith_shift_right, HB - 1, ALU.bitwise_and)
             lb, l0 = "hu", c0
             vec("tensor_copy", R(lb, c0, c1), h[4])
-            w0, ck = 16 * c0, 16 * nc // NZ
-            if any(x != "pe" for x in CFG["how"][t][s]):
-                for i in range(NZ):
-                    mms([(R(zb[i], 0, ck), DT, R("rr", i * ck, (i + 1) * ck, 1, 0, nc))])
-                    act(R("drep", w0 + i * ck, w0 + (i + 1) * ck), R(zb[i], 0, ck), ACT.Copy)
+            together(False)
+            w0, n0 = 16 * c0, 3 * c0
+            xs = CFG["xp"][t][s]
+            nr, i, k = max(sum(n for n, h in p if h != "pe") for p in xs), 0, 0
+            if CFG["gd"] and nr:
+                def rep(j0, j1, a=c0, b=c0 + nr):
+                    return ("3", "drep3", 0, 128, 16 * a, 16 * b, 1 if j1 - j0 == 16 else 2, j0, j1)
+                for o, x in [(rep(j, j + 1), R("dsb", D[4], D[4] + nr)) for j in range(2)] + [(rep(j, 2 * j), rep(0, j)) for j in (2, 4, 8)]:
+                    pat = [[0, nr]] + ([[0, o[8] - o[7]]] if o[8] - o[7] > 1 else [])
+                    add("g", [("affine_select", (o, x, pat, ALU.is_ge, 0.0, 0, 0), {})], ("as", cols(o)))
+            while i < nr and not CFG["gd"]:
+                n = min(nr - i, 32 if nr <= 32 else nr // 2)
+                pz = R(zb[k], 0, 16 * n)
+                mms([(pz, DT, R("rr", 16 * i, 16 * (i + n), 1, 0, nc))])
+                copy(R("drep", w0 + 16 * i, w0 + 16 * (i + n)), pz)
+                i, k = i + n, k + 1
+            sx = CFG["sx"][t][s]
             for l in range(3):
-                gl, gx, zz = "gl%d" % l, "gx%d" % l, "zz%d" % l
-                le = CFG["le"][t][s][l]
-                n = nc // len(le)
-                for i, e in enumerate(le):
-                    copy(e, R(gl, w0 + 16 * n * i, w0 + 16 * n * (i + 1)), IND(R("hdw") if l == 0 else R("nxw"), R(lb, l0 + n * i, l0 + n * (i + 1))))
-                pa = R(Pb, p0 + (1 + l) * nc, p0 + (2 + l) * nc)
-                mms([(pa, R("ed", 128 * d, 128 * d + 128), R(gl, w0 + d, w0 + 16 * nc, 16)) for d in range(16)])
+                gl, i, x0 = "gl%d" % l, 0, 3 * w0 + 16 * nc * l
+                for n in CFG["lp"][t][s][l]:
+                    G = R(gl, w0 + 16 * i, w0 + 16 * (i + n))
+                    copy(G, IND(R("hdw", 0, HB) if l == 0 else R("nxw"), R(lb, l0 + i, l0 + i + n)))
+                    if sx[l]:
+                        vec("tensor_tensor_scan", R("sl", x0 + 16 * i, x0 + 16 * (i + n)), G, R("cx", 0, 16 * n), -1.0, ALU.max, ALU.add)
+                    i += n
                 lb, l0 = "off", 3 * c0 + l * nc
-                vec("tensor_copy", R(lb, l0, l0 + nc), pa)
-                how, xe = CFG["how"][t][s][l], CFG["xe"][t][s][l]
-                n = nc // len(xe)
-                for i, e in enumerate(xe):
-                    G, a = R(gx, w0 + 16 * n * i, w0 + 16 * n * (i + 1)), IND(xwin, R(lb, l0 + n * i, l0 + n * (i + 1)))
+                if sx[l]:
+                    ts(R(lb, l0, l0 + nc), R("sl", x0 + 15, x0 + 16 * nc, 16), float(V), ALU.add)
+                else:
+                    pa = R(Pb, (1 + l) * nc, (2 + l) * nc)
+                    mms([(pa, R("ed", 128 * d, 128 * d + 128), R(gl, w0 + d, w0 + 16 * nc, 16)) for d in range(16)])
+                    ts(R(lb, l0, l0 + nc), pa, -1.0, ALU.mult)
+                    if l == 2 or sx[l + 1]:
+                        a = min(j for j in range(l + 1) if not any(sx[j:l + 1]))
+                        o, x = R("sl", x0 + 15 - 16 * nc * (l - a), x0 + 16 * nc, 16), R(Pb, (1 + a) * nc, (2 + l) * nc)
+                        ts(o, x, -1.0, ALU.mult, -float(V), ALU.add, alt=actf(o, x, ACT.Identity, scale=-1.0, bias=-float(V)))
+                i, half = 0, any(how == "relu" for j in range(3) for n, how in xs[j] if j == l or (CFG["msum"][t][s] and j < 2 and l < 2))
+                kw = {"scale": 0.5} if half else {}
+                for n, how in xs[l]:
+                    G, a = R("gx", x0 + 16 * i, x0 + 16 * (i + n)), IND(xwin, R(lb, l0 + i, l0 + i + n))
+                    Z = R("zz", G[4], G[5])
                     if how == "pe":
-                        copy(e, G, a)
+                        copy(G, a)
+                        k += 1
+                        pz = R(zb[k % NZ], 0, 16 * n)
+                        two = [(pz, DT, R("rr", 16 * i, 16 * (i + n), 1, 0, nc)), (pz, R("nidb"), G)]
+                        if CFG["pre"]:
+                            mms(two[:1], stop=False)
+                            mms(two[1:], start=False)
+                        else:
+                            mms(two)
+                        act(Z, pz, ACT.Abs, **kw)
                     else:
-                        tt(G, a, R("drep", G[4], G[5]), ALU.subtract)
-                        Z = R(zz, G[4], G[5])
+                        tt(G, a, rep(0, 16, c0 + i, c0 + i + n) if CFG["gd"] else R("drep", w0 + 16 * i, w0 + 16 * (i + n)), ALU.subtract)
                         if how == "abs":
-                            act(Z, G, ACT.Abs)
+                            act(Z, G, ACT.Abs, **kw)
                         else:
                             ts(Z, G, 0.0, ALU.max)
-                if how == "pe":
-                    for i in range(NZ):
-                        pz = R(zb[i], 0, ck)
-                        mms([(pz, DT, R("rr", i * ck, (i + 1) * ck, 1, 0, nc)), (pz, R("nidb"), R(gx, w0 + i * ck, w0 + (i + 1) * ck))])
-                        act(R(zz, w0 + i * ck, w0 + (i + 1) * ck), pz, ACT.Abs)
-                pq = R(Qb, q0 + l * nc, q0 + (l + 1) * nc)
-                parts = (("bn", gx), ("b2", zz)) if how == "relu" else (("b1", zz),)
-                mms([(pq, R(bn, 15 - d, 143 - d), R(bf, w0 + d, w0 + 16 * nc, 16)) for bn, bf in parts for d in range(16)])
-            n0 = 3 * c0
-            cand = R("cand", n0, n0 + 3 * nc)
-            vec("tensor_copy", cand, R("off", n0, n0 + 3 * nc))
-            ts(R("near", n0, n0 + 3 * nc), R(Qb, q0, q0 + 3 * nc), R("thf", 0, 1), ALU.is_le)
-            pv = R(Qb, q0 + 3 * nc, q0 + 6 * nc)
-            mms([(pv, R("nidh"), cand),
-                 (R(Qb, q0 + 4 * nc, q0 + 6 * nc), R("o4h"), R("near", n0, n0 + 2 * nc)),
-                 (R(Qb, q0 + 5 * nc, q0 + 6 * nc), R("o4h"), R("near", n0, n0 + nc)),
-                 (pv, R("trih"), R("near", n0, n0 + 3 * nc))])
-            ts(R("yy", n0, n0 + 3 * nc), pv, -float(V), ALU.add, 0.0, ALU.max)
-            mms([(R(Qb, q0 + 6 * nc, q0 + 7 * nc), R("oneh"), R("yy", n0 + l * nc, n0 + (l + 1) * nc)) for l in range(3)])
+                    i += n
+                m = 1 if CFG["msum"][t][s] and l < 2 else 0
+                if not (m and l == 0):
+                    pq = R(Qb, (l - m) * nc, (l + 1) * nc)
+                    grp = [(pq, R("b2" if half else "b1", 15 - d, 143 - d), R("zz", x0 - 16 * nc * m + d, x0 + 16 * nc, 16)) for d in range(16)]
+                    runs, i = [], (l - m) * nc
+                    for n, how in [p for j in range(l - m, l + 1) for p in xs[j]]:
+                        if how == "relu":
+                            if runs and runs[-1][1] == i:
+                                runs[-1][1] = i + n
+                            else:
+                                runs.append([i, i + n])
+                        i += n
+                    for a, b in runs:
+                        grp += [(R(Qb, a, b), R("bn", 15 - d, 143 - d), R("gx", 3 * w0 + 16 * a + d, 3 * w0 + 16 * b, 16)) for d in range(16)]
+                    mms(grp)
+
+            def lv(name, a, b):
+                return R(name, n0 + a * nc, n0 + b * nc)
+
+            def pv(a, b):
+                return R(Pb, 5 * nc, 6 * nc) if a == 2 else R(Qb, (3 + a) * nc, (3 + b) * nc)
+
+            def cand(a, b):
+                c = [(pv(a, b), R("nidh"), R("sl", 3 * w0 + 16 * nc * a + 15, 3 * w0 + 16 * nc * b, 16))]
+                return c + ([(pv(a, b), R("idb"), R("base", a * nc, b * nc))] if CFG["sign"] else [])
+
+            def near(a, b):
+                if CFG["sign"]:
+                    act(lv("near", a, b), R(Qb, a * nc, b * nc), ACT.Sign, scale=-1.0, bias=R("thf", 1, 2))
+                else:
+                    ts(lv("near", a, b), R(Qb, a * nc, b * nc), R("thf", 0, 1), ALU.is_le)
+
+            def first(a, b):
+                c = -float(V) if CFG["sign"] else -2.0 * V
+                ts(lv("yy", a, b), pv(a, b), c, ALU.add, 0.0, ALU.max, alt=actf(lv("yy", a, b), pv(a, b), ACT.Relu, bias=c))
+            if CFG["early"][t][s]:
+                near(0, 2)
+                mms(cand(0, 2) + [(pv(1, 2), o4n, lv("near", 0, 1)), (pv(0, 2), R("trih"), lv("near", 0, 2))])
+                first(0, 2)
+                mms(cand(2, 3) + [(pv(2, 3), o4n, lv("near", l, l + 1)) for l in range(2)], stop=False)
+                near(2, 3)
+                mms([(pv(2, 3), R("trih"), lv("near", 2, 3))], start=False)
+                first(2, 3)
+            else:
+                near(0, 3)
+                mms(cand(0, 3) + [(pv(1, 3), o4n, lv("near", 0, 2)), (R(Qb, 5 * nc, 6 * nc), o4n, lv("near", 0, 1)),
+                                  (pv(0, 3), R("trih"), lv("near", 0, 3))])
+                first(0, 3)
+            mms([(R(Qb, 6 * nc, 7 * nc), R("oneh"), lv("yy", l, l + 1)) for l in range(3)])
         for s, (c0, c1) in enumerate(STREAMS):
             nc = c1 - c0
-            tag[0] = CFG["bias"][t][s]
-            K, k0 = nc // 16, c0 // 16
-            (Pb, p0), (Qb, q0), zb = CFG["banks"][s]
+            tag[0] = NS * t + s
+            K = nc // 16
+            Pb, Qb, zb = CFG["banks"][s]
             D = R("dsb", t * CH + c0, t * CH + c1)
-            pq = R(Qb, q0 + 6 * nc, q0 + 7 * nc)
-            m, hold = R("mm", c0, c1), R("hold", c0, c1)
+            pq = R(Qb, 6 * nc, 7 * nc)
+            m = R("mm", t * CH + c0, t * CH + c1)
+            ow, z, pw = R("offw", 8 * s, 8 * s + K), R("zs", c0, c1), R(Pb, 0, nc)
+            h0 = 128 * s + 64
+            hold, pl, es = R("hold", h0, h0 + nc), [] if s == 0 else [(pw, R("nidh"), z)], []
+            together()
             tt(m, R(mask, 0, nc), pq, ALU.mult)
             vec("tensor_tensor_scan", hold, R("nmask", 0, nc), m, 0.0, ALU.mult, ALU.add)
-            ow = R("offw", 8 * s, 8 * s + K)
-            ts(ow, R("hold", c0 + 15, c1, 16), -1.0, ALU.mult, float(V), ALU.add)
-            z = R("zs", c0, c1)
-            tt(z, IND(xwin, ow), D, ALU.subtract)
-            pl = [(R(Pb, p0, p0 + nc), R("idb"), z)]
-            for k in range(K):
-                n = nc - 16 * k - 1
+            for k in range(K - 1, -1, -1):
+                n = nc if k == K - 1 else nc - 16 * k - 1
                 e = R("ee", 4 * c0 + k * nc, 4 * c0 + k * nc + n)
-                tt(e, R("hold", c0, c0 + n), R(Qb, q0 + 7 * nc - n, q0 + 7 * nc), ALU.is_equal)
-                pl.append((R(Pb, p0 + nc - n, p0 + nc), R("kblk"), e))
-            ts(R("dl", c0, c1), z, 0.25, ALU.mult, -0.375, ALU.add)
+                tt(e, R("hold", h0 + nc - 16 * k - 1 - n, h0 + nc - 16 * k - 1), R(Qb, 7 * nc - n, 7 * nc), ALU.is_equal)
+                es.append((n, e))
+            pl += [(R(Pb, nc - n, nc), R("o4h"), e) for n, e in es]
+            together(False)
+            if t < RO - 1 or s < NS - 1:
+                pt = R(Pb, 4 * nc, 5 * nc)
+                mms([(pt, R("nidh"), R("ct", 0, nc)), (pt, R("idh"), m)] + [(R(Pb, 5 * nc - n, 5 * nc), R("o4h"), e) for n, e in es])
+            together()
+            ts(ow, R("hold", h0 + 15, h0 + nc, 16), -1.0, ALU.mult, float(V), ALU.add)
+            tt(z, IND(xwin, ow), D, ALU.subtract)
+            together(s == 0)
+            run[0] *= 2
+            dl = R("dl", c0, c1)
+            ts(dl, z, 0.25, ALU.mult, -0.375, ALU.add)
+            together(False)
             mms(pl)
-            w = R("ww", c0, c1)
-            ts(w, R(Pb, p0, p0 + nc), 256.0, ALU.is_lt)
+            w = R("ww", t * CH + c0, t * CH + c1)
+            together()
+            ts(w, pw, -256.0, ALU.is_gt)
             dw = R("dw", t * CH + c0, t * CH + c1)
-            tt(dw, R("dl", c0, c1), w, ALU.mult)
+            tt(dw, dl, w, ALU.mult)
             if t == RO - 1:
                 tt(R("cf", c0, c1), dw, D, ALU.add)
+                together(False)
                 send(t, R("landf", c0, c1), R("cf", c0, c1))
                 dma("y", ("d", "yc", (c0, c1)), R("landf", c0, c1), 128 * nc * 4)
-            elif CFG["split"]:
-                send(t, R("lande", t * CH + c0, t * CH + c1), dw)
             else:
-                cn = R("cn", t * CH + c0, t * CH + c1)
-                tt(cn, dw, D, ALU.add)
-                send(t, R("landd", t * CH + c0, t * CH + c1), cn)
-            tt(R("mq", c0, c1), m, R("maskc", c0, c1), ALU.add)
-            m2c = t * CH + c0
-            tt(R("m2", m2c, m2c + nc), R("mq", c0, c1), w, ALU.mult)
+                if not CFG["split"][t]:
+                    tt(R("cn", t * CH + c0, t * CH + c1), dw, D, ALU.add)
+                    dw = R("cn", t * CH + c0, t * CH + c1)
+                together(False)
+                send(t, R("lande", t * CH + c0, t * CH + c1), dw)
             if t < RO - 1 or s < NS - 1:
-                of = R("offf", k0, k0 + K)
-                if CFG["tomb_s"]:
-                    for k in range(K):
-                        act(R("junk", c0 + 16 * k, c0 + 16 * k + 16), R("m2", m2c + 16 * k, m2c + 16 * k + 16), ACT.Identity, scale=-1.0,
-                            bias=R("bc", k0 + k, k0 + k + 1), accum_out=R("offf", k0 + k, k0 + k + 1))
-                else:
-                    vec("tensor_tensor_scan", R("hold2", c0, c1), R("nmask", 0, nc), R("m2", m2c, m2c + nc), 0.0, ALU.mult, ALU.add)
-                    tt(of, R("bc", k0, k0 + K), R("hold2", c0 + 15, c1, 16), ALU.subtract)
+                together()
+                vec("tensor_tensor_scan", R("hold2", c0, c1), R("maskd", c0, c1), pt, 0.0, ALU.min, ALU.max)
                 ot = R("offt", 8 * s, 8 * s + K)
-                vec("tensor_copy", ot, of)
+                ts(ot, R("hold2", c0 + 15, c1, 16), -1.0, ALU.mult)
+                together(False)
                 vec("tensor_copy", IND(xwin, ot), R("c512", 0, nc))
+    tag[0] = "e"
     yb = CFG["banks"][0][2][0]
     for t in range(RO):
         o = R(yb, t * CH, (t + 1) * CH, 1, 0, 8)
-        mms([(o, R("g8"), R("maskd")), (o, R("g8n"), R("m2", t * CH, (t + 1) * CH))])
-    ts(R("yts", 0, RO * CH, 1, 0, 8), R(yb, 0, RO * CH, 1, 0, 8), float(V), ALU.min)
+        mms([(o, R("g8a"), R("mm", t * CH, (t + 1) * CH)), (o, R("g8b"), R("ww", t * CH, (t + 1) * CH))])
+    ts(R("yts", 0, RO * CH, 1, 0, 8), R(yb, 0, RO * CH, 1, 0, 8), 6144.0, ALU.add, float(V), ALU.min)
     dma("s", ("d", "yt", None), R("yts", 0, RO * CH, 1, 0, 8), 8 * RO * CH * 4)
     return ops
 
 
 MODELS = [
-    {"f": 1.05, "g": 1.15, "sc": 2.0, "pe": 0.44, "pm": 0, "hx": 70, "hs": 50, "ri": 400, "rl": 1800, "bw": 350.0},
-    {"f": 1.25, "g": 1.56, "sc": 3.8, "pe": 0.52, "pm": 0, "hx": 100, "hs": 70, "ri": 700, "rl": 2500, "bw": 250.0},
-    {"f": 1.4, "g": 2.0, "sc": 5.5, "pe": 0.6, "pm": 0, "hx": 130, "hs": 90, "ri": 1000, "rl": 3200, "bw": 180.0},
+    {"f": 1.06, "g": 1.2, "tt": 2.4, "sc": 3.0, "pe": 0.5, "pm": 0, "pl": 100, "sf": 30, "hx": 170, "hs": 70, "ri": 900, "rt": 1100, "rl": 2300, "bw": 450.0, "unit": 58.0},
+    {"f": 1.08, "g": 1.3, "tt": 2.4, "sc": 3.8, "pe": 0.45, "pm": 3, "pl": 120, "sf": 30, "hx": 200, "hs": 110, "ri": 800, "rt": 1300, "rl": 2700, "bw": 450.0, "unit": 62.0},
+    {"f": 1.06, "g": 1.4, "tt": 2.6, "sc": 3.8, "pe": 0.49, "pm": 6, "pl": 110, "sf": 80, "hx": 140, "hs": 105, "ri": 600, "rt": 800, "rl": 2850, "bw": 550.0, "unit": 62.0},
+    {"f": 1.4, "g": 1.8, "tt": 2.8, "sc": 5.5, "pe": 0.6, "pm": 8, "pl": 120, "sf": 60, "hx": 180, "hs": 160, "ri": 900, "rt": 1300, "rl": 3000, "bw": 500.0, "unit": 82.0},
 ]
-UNIT = [55.0, 70.0, 90.0]
 ENG = {"v": 0, "s": 1, "t": 2, "g": 3, "y": 4, None: 5}
+OTHERS = [(1, 2), (0, 2), (0, 1)]
+STRIDE = 24
 
 
-def times(op, m):
-    c = op["cost"]
+def times(c, m):
     k = c[0]
-    if k in ("v", "s"):
-        d = max(64, c[1]) * 0.83 * m["f"]
+    if k == "run":
+        d = times(c[1], m)[0] + times(c[2], m)[0] + c[3] * m["hs"]
+    elif k in ("v", "s"):
+        d = max(64, c[1]) * 0.83 * m["f"] + (m["sf"] if k == "s" else 0)
     elif k == "g":
-        d = (55 + c[1] * m["g"] * 0.83) * m["f"]
+        d = (50 + c[1] * m["g"] * 0.83) * m["f"]
+    elif k == "gt":
+        d = (50 + c[1] * max(m["g"], m.get("tt", 1.8)) * 0.83) * m["f"]
+    elif k == "gs":
+        d = (65 + c[1] * m["g"] * 0.83) * m["f"] + m["sf"]
     elif k == "sc":
         d = (50 + c[1] * m["sc"] * 0.83) * m["f"]
     elif k == "t":
-        d = c[1] * m["pe"] + 30 + c[2] * m["pm"]
+        d = c[1] * m["pe"] + c[2] * m["pm"]
+        return d, d + m["pl"]
     elif k == "io":
         d = (130 + 2 * c[1] * 0.83) * m["f"]
+    elif k == "as":
+        d = (170 + 2 * c[1] * 0.83) * m["f"]
     elif k == "dma":
         return 60, 1600
     elif k == "r":
         return m["ri"], m["ri"]
     else:
-        return 0, m["rl"] - m["ri"]
+        return 0, m["rl"] - m["ri"] - m["rt"]
     return d, d
 
 
 def table(ops, m):
     tb = []
     for op in ops:
-        e, dl = op["eng"], []
-        for o, k in op["deps"].items():
-            p = ops[o]
-            if k == "ord":
-                if e is None:
-                    dl.append((o, 0))
-            elif p["eng"] != e or p["kind"] != "c" or op["kind"] != "c":
-                dl.append((o, m["hx"]))
-            else:
-                dl.append((o, m["hs"]))
-        hold, lat = times(op, m)
-        tb.append((ENG[e], hold, lat, op["cost"][1] / m["bw"] if op["kind"] == "dma" else -1, dl, [int(b[2]) for b in op["banks"]]))
-    return tb, m["hx"]
+        cc = [o for o, k in op["deps"].items() if k != "ord" and ops[o]["kind"] == "c" and op["kind"] == "c"]
+        xx = [(o, 0 if k == "ord" else m["hx"]) for o, k in op["deps"].items() if o not in cc and (k != "ord" or op["eng"] is None)]
+        tb.append(({ENG[e]: times(f[1], m) for e, f in op["forms"].items()},
+                   op["cost"][1] / m["bw"] if op["kind"] == "dma" and op["cost"][1] > 30000 else m["rt"] if op["kind"] == "rdma" else -1, cc, xx,
+                   [3 * int(b[2]) for b in op["banks"]]))
+    return tb, m["hx"], m["hs"]
 
 
-def fresh(n):
-    return [[0.0] * 6, [0.0] * n, [[-1e9] * 3 for b in range(8)], [0.0]]
+def replay(tab, order, eng, p0=0, old=None, upto=None):
+    tb, hx, hs = tab
+    n = len(tb)
+    if old is None or p0 < STRIDE:
+        p0, q, fin, bank, dq, lq, why, bl, snaps = 0, [0.0] * 6, [0.0] * n, [-1e9] * 24, 0.0, [-1] * 6, [-1] * n, [-1] * 24, [None]
+    else:
+        k = p0 // STRIDE
+        p0, fin, why, snaps = k * STRIDE, old[0][:], old[1][:], old[2][:k + 1]
+        q, bank, lq, bl, dq = snaps[k]
+        q, bank, lq, bl = q[:], bank[:], lq[:], bl[:]
+    nxt = p0 + STRIDE
+    for p in range(p0, n):
+        if p == nxt:
+            snaps.append((q[:], bank[:], lq[:], bl[:], dq))
+            nxt += STRIDE
+        i = order[p]
+        fm, dm, cc, xx, bk = tb[i]
+        e = eng[i]
+        s, w = q[e], lq[e]
+        for o in cc:
+            x = fin[o] + (hs if eng[o] == e else hx)
+            if x > s:
+                s, w = x, o
+        for o, d in xx:
+            x = fin[o] + d
+            if x > s:
+                s, w = x, o
+        hold, lat = fm[e]
+        if bk:
+            for b in bk:
+                for e2 in OTHERS[e]:
+                    x = bank[b + e2] + hx
+                    if x > s:
+                        s, w = x, bl[b + e2]
+            for b in bk:
+                bank[b + e], bl[b + e] = s + lat, i
+        f = s + lat
+        if dm >= 0:
+            f = dq = max(f, dq) + dm
+        fin[i], why[i] = f, w
+        if e < 5:
+            q[e], lq[e] = s + hold, i
+    return fin, why, snaps
 
 
-def place(tab, i, st):
-    tb, hx = tab
-    e, hold, lat, dm, dl, bk = tb[i]
-    s, fin = st[0][e], st[1]
-    for o, d in dl:
-        if fin[o] + d > s:
-            s = fin[o] + d
-    for b in bk:
-        x = st[2][b]
-        for e2 in (0, 1, 2):
-            if e2 != e and x[e2] + hx > s:
-                s = x[e2] + hx
-    return s
+def first_order(ops, succ):
+    n = len(ops)
+    tb, hx, hs = table(ops, MODELS[1])
+    due, dead = [0.0] * n, CFG["dead"]
+    for i in range(n - 1, -1, -1):
+        d = min([due[j] - hx for j in succ[i]], default=dead[-1] + 4000)
+        if ops[i]["kind"] == "rdma" and ops[i]["ins"][0][1][0][1] != "landd":
+            d = min(d, dead[ops[i]["ph"]])
+        due[i] = d - min(v[1] for v in tb[i][0].values()) - max(tb[i][1], 0)
+    q, fin, bank, dq, eng = [0.0] * 6, [0.0] * n, [-1e9] * 24, 0.0, [5] * n
+    left = [len(op["deps"]) for op in ops]
+    ready, order = [i for i in range(n) if left[i] == 0], []
 
-
-def commit(tab, i, st, s):
-    e, hold, lat, dm, dl, bk = tab[0][i]
-    f = s + lat
-    if dm >= 0:
-        f = st[3][0] = max(f, st[3][0]) + dm
-    st[1][i] = f
-    if e < 5:
-        st[0][e] = s + hold
-    for b in bk:
-        st[2][b][e] = f
-
-
-def replay(tab, order):
-    st = fresh(len(order))
-    for i in order:
-        commit(tab, i, st, place(tab, i, st))
-    return max(st[1]) + 0.05 * sum(st[1]) / len(order)
+    def start(i, e):
+        fm, dm, cc, xx, bk = tb[i]
+        return max([q[e]] + [fin[o] + (hs if eng[o] == e else hx) for o in cc] + [fin[o] + d for o, d in xx]
+                   + [bank[b + e2] + hx for b in bk for e2 in OTHERS[e]])
+    while ready:
+        ss = [min((start(i, e) + f[1], start(i, e), i, e) for e, f in tb[i][0].items())[1:] for i in ready]
+        s0, i0, e0 = min(ss)
+        s, i, e = min([c for c in ss if c[0] <= s0 + CFG["win"] and c[2] == e0], key=lambda c: due[c[1]] + 2 * (c[0] - s0))
+        fm, dm, cc, xx, bk = tb[i]
+        fin[i], eng[i] = s + fm[e][1], e
+        if dm >= 0:
+            fin[i] = dq = max(fin[i], dq) + dm
+        if e < 5:
+            q[e] = s + fm[e][0]
+        for b in bk:
+            bank[b + e] = fin[i]
+        order.append(i)
+        ready.remove(i)
+        for j in succ[i]:
+            left[j] -= 1
+            if left[j] == 0:
+                ready.append(j)
+    return order, eng
 
 
 def schedule(ops):
     n = len(ops)
-    succ = [[] for i in range(n)]
+    succ = [set() for i in range(n)]
     for i, op in enumerate(ops):
         for o in op["deps"]:
-            succ[o].append(i)
-    tabs = [table(ops, m) for m in MODELS]
-    tab = tabs[1]
-    lev = [0.0] * n
-    for i in range(n - 1, -1, -1):
-        lev[i] = tab[0][i][2] + max(tab[0][i][3], 0) + max([lev[j] + tab[1] for j in succ[i]], default=0.0)
+            succ[o].add(i)
+    order, eng = CFG.get("init", first_order)(ops, succ)
+    tabs = [(table(ops, MODELS[k]), MODELS[k]["unit"]) for k in CFG["models"]]
+    flex = [len(op["forms"]) > 1 for op in ops]
     x = [CFG["seed"]]
 
     def rnd():
         x[0] = (x[0] * 1103515245 + 12345) % 2147483648
         return x[0] / 2147483648.0
 
-    def decode(pr, win):
-        st = fresh(n)
-        left = [len(op["deps"]) for op in ops]
-        ready = [i for i in range(n) if left[i] == 0]
-        order = []
-        while ready:
-            ss = [(place(tab, i, st), i) for i in ready]
-            s0, i0 = min(ss)
-            e0 = tab[0][i0][0]
-            s, i = max([c for c in ss if c[0] <= s0 + win and tab[0][c[1]][0] == e0], key=lambda c: pr[c[1]] - 2 * (c[0] - s0))
-            commit(tab, i, st, s)
-            order.append(i)
-            ready.remove(i)
-            for j in succ[i]:
-                left[j] -= 1
-                if left[j] == 0:
-                    ready.append(j)
-        return order
-    best = None
-    for it in range(CFG["tries"]):
-        jit = 1500 * rnd() ** 2
-        order = decode([v + jit * rnd() + op["bias"] for v, op in zip(lev, ops)], 1000 * rnd())
-        sc = [replay(tb, order) for tb in tabs]
-        v = sum(a / b for a, b in zip(sc, UNIT))
-        if best is None or v < best[0]:
-            best = (v, order, sc)
+    def value(o, e, p0, old):
+        res = [replay(t, o, e, p0, old[k] if old else None) for k, (t, u) in enumerate(tabs)]
+        return sum((max(r[0]) + 0.05 * sum(r[0]) / n + sum(w * r[0][i] for i, w in moves)) / u for r, (t, u) in zip(res, tabs)) * 3 / len(tabs), res
+    moves = [i for i in range(n) if ops[i]["kind"] == "rdma" and ops[i]["ins"][0][1][0][1] != "landd"]
+    moves = list(zip(moves, CFG["pull"]))
+
+    def path(res):
+        arcs = []
+        for f, why, sn in res:
+            i = f.index(max(f)) if rnd() < 0.5 else moves[int(rnd() * len(moves))][0]
+            while why[i] >= 0:
+                if i not in succ[why[i]]:
+                    arcs.append((why[i], i))
+                elif flex[i]:
+                    arcs.append((-1, i))
+                i = why[i]
+        return arcs
+
+    def move(k, j):
+        d = 1 if j > k else -1
+        carry = [order[k]]
+        for p in range(k + d, j + d, d):
+            y = order[p]
+            if any(y in succ[c] for c in carry) if d > 0 else any(c in succ[y] for c in carry):
+                carry.append(y)
+        if order[j] in carry:
+            return None
+        lo, hi = min(j, k), max(j, k)
+        a = [y for y in order[lo:hi + 1] if y in carry]
+        b = [y for y in order[lo:hi + 1] if y not in carry]
+        return order[:lo] + (b + a if d > 0 else a + b) + order[hi + 1:]
+    cur = value(order, eng, 0, None)
+    best, arcs = (cur[0], order, eng), path(cur[1])
+    steps = CFG["steps"]
+    for it in range(steps):
+        o2, e2, r = order, eng, rnd()
+        if it % 16 == 0:
+            arcs = path(cur[1])
+        if r < 0.75 and arcs:
+            u, v = arcs[int(rnd() * len(arcs))]
+            r2 = rnd()
+            if u < 0 or (r2 < 0.3 and (flex[u] or flex[v])):
+                i = v if u < 0 or not flex[u] or (flex[v] and rnd() < 0.5) else u
+                e2 = eng[:]
+                e2[i] ^= 1
+                p0 = k = order.index(i)
+                if rnd() < 0.4:
+                    c = [y for y in order[max(0, k - 10):k + 10] if flex[y] and eng[y] == e2[i]]
+                    if c:
+                        e2[c[int(rnd() * len(c))]] ^= 1
+                    p0 = max(0, k - 10)
+            else:
+                p0, kv = order.index(u), order.index(v)
+                o2 = move(kv, p0) if r2 < 0.65 else move(p0, kv)
+        else:
+            k = int(rnd() * n)
+            d, j, cnt = (1 if rnd() < 0.5 else -1), k, 1 + int(rnd() ** 2 * 3)
+            while cnt and 0 <= j + d < n:
+                j += d
+                cnt -= eng[order[j]] == eng[order[k]]
+            o2, p0 = (None if cnt else move(k, j)), min(k, j)
+        if o2 is None:
+            continue
+        new = value(o2, e2, p0, cur[1])
+        heat = CFG["heat"] * (1 - it / steps) ** 2 + 0.05
+        if new[0] <= cur[0] or rnd() < math.exp((cur[0] - new[0]) / heat):
+            cur, order, eng = new, o2, e2
+            arcs = path(cur[1])
+            if new[0] < best[0]:
+                best = (new[0], o2, e2)
     return best
 
 
 def plan():
     ops = build()
-    v, order, sc = schedule(ops)
+    v, order, eng = schedule(ops)
+    for op, e in zip(ops, eng):
+        if len(op["forms"]) > 1:
+            op["eng"] = "vs"[e]
+            op["ins"], op["cost"] = op["forms"][op["eng"]]
     place_of = {o: k for k, o in enumerate(order)}
     pos, cnt = {}, {}
     known = {e: {} for e in "vstgy"}
@@ -540,7 +766,7 @@ def plan():
             clock[i][e] = cnt[e]
         else:
             clock[i][("x", i)] = 1
-    return ops, order, waits, need, sc
+    return ops, order, waits, need, eng
 
 
 PLAN = []
@@ -552,7 +778,7 @@ def rank_program(g, core, T, topo):
         return
     if not PLAN:
         PLAN.append(plan())
-    ops, order, waits, need, sc = PLAN[0]
+    ops, order, waits, need, eng = PLAN[0]
     dst = [T.cores[(rank + 1 + t % (N - 1)) % N] for t in range(RO)]
     src = [T.cores[(rank - 1 - t % (N - 1)) % N] for t in range(RO)]
 
@@ -571,6 +797,8 @@ def rank_program(g, core, T, topo):
             return A(a[1]).indirect(A(a[2]))
         if a[0] == "d":
             return T[a[1]][:] if a[2] is None else T[a[1]][:, a[2][0]:a[2][1]]
+        if a[0] == "3":
+            return T[a[1]][:, a[4] // 16:a[5] // 16, a[7] if a[8] - a[7] == 1 else slice(a[7], a[8])]
         if a[6] == 1:
             return T[a[1]][a[2]:a[3], a[4]:a[5]]
         return T[a[1]][a[2]:a[3], a[4]:a[5]:a[6]]
@@ -592,6 +820,11 @@ def rank_program(g, core, T, topo):
             sent += bin(lanes(core)).count("1")
             continue
         for m, args, kw in op["ins"]:
+            if m == "wait":
+                cnt[e] = cnt.get(e, 0) + 1
+                ins.then_inc(T.sem["q" + e], 1)
+                q.wait_ge(T.sem["q" + e], cnt[e])
+                continue
             ins = CALL[m](q, [A(x) for x in args], {n: A(x) for n, x in kw.items()})
         if op["kind"] == "dma":
             ins.then_inc(T.sem[op["x"]], 16)
@@ -616,5 +849,6 @@ CALL = {
     "tensor_tensor_scan": lambda q, a, k: q.tensor_tensor_scan(*a),
     "memset": lambda q, a, k: q.memset(*a),
     "iota": lambda q, a, k: q.iota(*a, **k),
+    "affine_select": lambda q, a, k: q.affine_select(*a),
     "dma_start": lambda q, a, k: q.dma_start(*a),
 }

@@ -3,17 +3,18 @@ from concourse.mybir import AluOpType as ALU, ActivationFunctionType as ACT
 
 V, HB, CH, RO, N = 2048, 4096, 96, 3, 8
 XW = V + 112
+FAR = 1024.0
 A_, P_ = "abs", "pe"
 CFG = {
     "streams": [(0, 48), (48, 96)],
     "banks": [("ps0", "ps1", ["ps4", "ps5"]), ("ps2", "ps3", ["ps6", "ps7"])],
     "lp": [[[[24, 24]] * 3] * 2] * 3,
-    "xp": [[[[(24, P_), (24, P_)]] * 3] * 2] * 3,
-    "early": [[0, 0]] * 3, "pre": 1, "sign": 0, "sq": 0, "sint": 0, "gd": 0, "join": 0, "split": [1, 1],
+    "xp": [[[[(24, "mx"), (24, "rs")], [(24, "mx"), (24, "rs")], [(24, "mx"), (24, "mx")]]] * 2] * 3,
+    "early": [[1, 1]] * 3, "pre": 1, "sign": 0, "sq": 0, "sint": 0, "gd": 0, "join": 0, "cross": 1, "tab": 0, "cl": 1, "tabfrom": 2, "split": [1, 1],
     "sx": [[[1, 1, 1]] * 2] * 3,
     "msum": [[0, 0]] * 3,
     "dead": [20000, 26500, 33000, 39500, 46000, 52500],
-    "win": 300, "seed": 2, "steps": 55000, "heat": 20.0, "pull": [0.3, 0.3, 0.3, 0.2, 0.1, 0.0], "models": [1, 3],
+    "win": 300, "seed": 3, "steps": 80000, "heat": 22.0, "pull": [0.3, 0.3, 0.3, 0.2, 0.1, 0.0], "models": [1, 3],
 }
 MAXS = 3
 
@@ -54,7 +55,9 @@ SCRATCH = {
     "offw": ("sbuf", [128, 8 * MAXS], "uint16"), "offt": ("sbuf", [128, 8 * MAXS], "uint16"),
     "ee": ("sbuf", [128, 4 * CH], "float16"), "zs": ("sbuf", [128, CH], "float16"), "dl": ("sbuf", [128, CH], "int32"),
     "ww": ("sbuf", [128, RO * CH], "float16"), "dw": ("sbuf", [128, RO * CH], "bfloat16"),
-    "cn": ("sbuf", [128, 2 * CH], "bfloat16"), "cf": ("sbuf", [128, CH], "float32"), "yts": ("sbuf", [128, RO * CH], "float32"),
+    "hdu": ("sbuf", [128, HB], "float32"), "ua": ("sbuf", [128, 256], "int32"), "ub": ("sbuf", [128, 256], "int32"),
+    "uc": ("sbuf", [128, 256], "int32"), "ul": ("sbuf", [128, 256], "uint16"),
+    "pob": ("sbuf", [128, 128], "bfloat16"), "nob": ("sbuf", [128, 128], "bfloat16"), "ex": ("sbuf", [128, 4 * CH], "float16"), "cn": ("sbuf", [128, 2 * CH], "bfloat16"), "cf": ("sbuf", [128, CH], "float32"), "yts": ("sbuf", [128, RO * CH], "float32"),
 }
 for b in range(8):
     SCRATCH["ps%d" % b] = ("psum", [128, 512], "float32")
@@ -203,7 +206,7 @@ def build():
     turn = 8 if CFG["sq"] else 0
     a = dma("y", R("c0b"), ("d", "c0", None), 24576)
     a = dma("y", R("hdw", turn, HB + turn), ("d", "hd", None), 128 * HB * 4, (a,))
-    for o, i, n in [(R("nxw", 0, V), ("d", "nx", None), 128 * V * 4), (R("xw", 0, V), ("d", "xr", None), 128 * V * 2)]:
+    for o, i, n in [(R("nxw", 0, V), ("d", "nx", None), 128 * V * 4), (R("xw", 0, V), ("d", "xr", None), 128 * V * 2)][::CFG.get("xf", 1)]:
         a = dma("y", o, i, n, (a,))
     a = dma("s", R("wtb"), ("d", "wt", None), 4096)
     if turn:
@@ -261,7 +264,12 @@ def build():
             ts(R("base", l * W // 16, (l + 1) * W // 16), R("deq", 0, W // 16), 0.0, ALU.mult, R("pf", 4 + l, 5 + l), ALU.add)
     o4n = R("o4n" if CFG["sign"] else "o4h")
     tt(R("trih"), R("tmpd"), o4n, ALU.mult)
-    bs = [("b1", 1.0)] if hows & {"pe", "abs"} else []
+    bs = [("b1", 1.0)] if hows & {"pe", "abs", "rl"} else []
+    if "rs" in hows:
+        copy(R("pob"), R("blk"))
+    if hows & {"rs", "mx"}:
+        bs += [("b2", 2.0), ("bn", -1.0)]
+        ts(R("nob"), R("blk"), -1.0, ALU.mult)
     if "relu" in hows:
         bs += [("b2", 2.0), ("bn", -1.0)]
     for nm, f in bs:
@@ -276,8 +284,10 @@ def build():
         ts(R("tmpc"), R("deq"), 4096.0, ALU.mult)
         tt(R("cx", 0, 128), R("tmpa"), R("tmpc"), ALU.add)
         ts(R("cx", 15, 128, 16), R("cx", 15, 128, 16), -6144.0, ALU.add)
-        for n in (128, 256, 512):
-            vec("tensor_copy", R("cx", n, 2 * n), R("cx", 0, n))
+        n, top = 128, 16 * max(x for a in CFG["lp"] for b in a for c in b for x in c)
+        while n < top:
+            copy(R("cx", n, min(2 * n, top)), R("cx", 0, min(n, top - n)))
+            n *= 2
     mask = "deq"
     together()
     ts(R("nmask"), R(mask, 0, CH), -1.0, ALU.mult, 1.0, ALU.add)
@@ -289,9 +299,10 @@ def build():
     ts(R("placed"), R("gcol", 0, CH), -16.0, ALU.mult, R("pf", 3, 4), ALU.add)
     tt(R("maskd"), R("placed"), R(mask, 0, CH), ALU.mult)
     together()
-    vec("memset", R("hold"), 0.0)
-    vec("memset", R("c512"), 512.0)
-    vec("memset", R("xw", V, XW), 512.0)
+    for s in range(NS):
+        vec("memset", R("hold", 128 * s, 128 * s + 64), 0.0)
+    vec("memset", R("c512"), FAR)
+    vec("memset", R("xw", V, XW), FAR)
     vec("memset", R("nxw", V, V + 8), V)
     together(False)
     vec("tensor_copy", R("thf", 0, 1), R("thi", 0, 1))
@@ -299,6 +310,21 @@ def build():
         ts(R("thf", 1, 2), R("thf", 0, 1), 0.5, ALU.add)
     if CFG["sq"]:
         vec("memset", R("thf", 2, 3), 16.0)
+
+    consts = [i for i, op in enumerate(ops) if op["kind"] == "c"]
+
+    def places(u, a, b, h):
+        ts(a, u, 32.0, ALU.add)
+        tt(b, u, a, ALU.mult)
+        ts(h, b, 5, ALU.arith_shift_right, HB - 1, ALU.bitwise_and)
+    if CFG["tab"]:
+        add("g", [("iota", (R("ua"), [[16, 256]], 0, 0), {})], ("io", 256))
+        ts(R("ua"), R("ua"), pd, ALU.add)
+        places(R("ua"), R("ub"), R("uc"), R("ub"))
+        vec("tensor_copy", R("ul"), R("ub"))
+        n = HB // CFG["tab"]
+        for i in range(0, HB, n):
+            copy(R("hdu", i, i + n), IND(R("hdw", 0, HB), R("ul", i // 16, (i + n) // 16)))
 
     xwin = R("xw")
     for t in range(RO):
@@ -310,7 +336,7 @@ def build():
             src = [R("c0b", c0, c1)] if t == 0 else [R(n, (t - 1) * CH + c0, (t - 1) * CH + c1) for n in ("landd", "lande")[1 - CFG["split"][t - 1]:]]
             D = R("dsb", t * CH + c0, t * CH + c1)
             DT = R("dtb", 128 * s, 128 * s + 128, 1, 0, nc)
-            ph = R(Pb, 0, nc)
+            ph = R(Pb, 7 * nc, 8 * nc)
             mms([(ph, R("wsh"), x) for x in src])
             pD, pDT = R(Qb, 0, nc), R(Qb, 3 * nc, 3 * nc + 128, 1, 0, nc)
             if not CFG["gd"] or any(h == "pe" for p in CFG["xp"][t][s] for n, h in p):
@@ -324,15 +350,15 @@ def build():
             vec("tensor_copy", h[0], ph)
             together()
             ts(h[1], h[0], HB - 1, ALU.bitwise_and)
-            ts(h[2], h[1], 32.0, ALU.add)
-            tt(h[3], h[1], h[2], ALU.mult)
-            ts(h[4], h[3], 5, ALU.arith_shift_right, HB - 1, ALU.bitwise_and)
+            heads = R("hdu") if CFG["tab"] and tag[0] >= CFG["tabfrom"] else R("hdw", 0, HB)
+            if heads[1] == "hdw":
+                places(*h[1:])
             lb, l0 = "hu", c0
-            vec("tensor_copy", R(lb, c0, c1), h[4])
+            vec("tensor_copy", R(lb, c0, c1), h[4 if heads[1] == "hdw" else 1])
             together(False)
             w0, n0 = 16 * c0, 3 * c0
             xs = CFG["xp"][t][s]
-            nr, i, k = max(sum(n for n, h in p if h != "pe") for p in xs), 0, 0
+            nr, i, k = max(sum(n for n, h in p if h not in ("pe", "rs", "mx")) for p in xs), 0, 0
             if CFG["gd"] and nr:
                 def rep(j0, j1, a=c0, b=c0 + nr):
                     return ("3", "drep3", 0, 128, 16 * a, 16 * b, 1 if j1 - j0 == 16 else 2, j0, j1)
@@ -345,12 +371,17 @@ def build():
                 mms([(pz, DT, R("rr", 16 * i, 16 * (i + n), 1, 0, nc))])
                 copy(R("drep", w0 + 16 * i, w0 + 16 * (i + n)), pz)
                 i, k = i + n, k + 1
-            sx = CFG["sx"][t][s]
+            sx, held = CFG["sx"][t][s], {}
+
+            def dist(a, b):
+                return R(Pb if a == 2 and CFG["early"][t][s] and xs[2][0][1] in ("rs", "mx") else Qb, a * nc, b * nc)
             for l in range(3):
                 gl, i, x0 = "gl%d" % l, 0, 3 * w0 + 16 * nc * l
                 for n in CFG["lp"][t][s][l]:
                     G = R(gl, w0 + 16 * i, w0 + 16 * (i + n))
-                    copy(G, IND(R("hdw", 0, HB) if l == 0 else R("nxw"), R(lb, l0 + i, l0 + i + n)))
+                    o = copy(G, IND(heads if l == 0 else R("nxw"), R(lb, l0 + i, l0 + i + n)))
+                    if t == 0 and l == CFG["cl"]:
+                        ops[o]["deps"] = {**{c: "ord" for c in consts}, **ops[o]["deps"]}
                     if sx[l]:
                         vec("tensor_tensor_scan", R("sl", x0 + 16 * i, x0 + 16 * (i + n)), G, R("cx", 0, 16 * n), -1.0, ALU.max, ALU.add)
                     i += n
@@ -370,17 +401,29 @@ def build():
                 for n, how in xs[l]:
                     G, a = R("gx", x0 + 16 * i, x0 + 16 * (i + n)), IND(xwin, R(lb, l0 + i, l0 + i + n))
                     Z = R("zz", G[4], G[5])
-                    if how == "pe":
+                    if how == "mx":
                         copy(G, a)
-                        k += 1
-                        pz = R(zb[k % NZ], 0, 16 * n)
+                        pz = R(zb[i > 0], 0, 16 * n)
+                        if held.get(pz[1]) != (i, n):
+                            held[pz[1]] = (i, n)
+                            mms([(pz, DT, R("rr", 16 * i, 16 * (i + n), 1, 0, nc))])
+                        tt(Z, G, pz, ALU.max)
+                    elif how in ("pe", "rl", "rs"):
+                        copy(G, a)
+                        pz = R(zb[i > 0], 0, 16 * n)
+                        held[pz[1]] = None
                         two = [(pz, DT, R("rr", 16 * i, 16 * (i + n), 1, 0, nc)), (pz, R("nidb"), G)]
                         if CFG["pre"]:
                             mms(two[:1], stop=False)
                             mms(two[1:], start=False)
                         else:
                             mms(two)
-                        act(Z, pz, ACT.Abs, **kw)
+                        if how == "rl":
+                            ts(Z, pz, 0.0, ALU.max, alt=actf(Z, pz, ACT.Relu))
+                        elif how == "rs":
+                            ts(Z, pz, -1.0, ALU.mult, 0.0, ALU.max, alt=actf(Z, pz, ACT.Relu, scale=-1.0))
+                        else:
+                            act(Z, pz, ACT.Abs, **kw)
                     else:
                         tt(G, a, rep(0, 16, c0 + i, c0 + i + n) if CFG["gd"] else R("drep", w0 + 16 * i, w0 + 16 * (i + n)), ALU.subtract)
                         if how == "abs":
@@ -389,8 +432,20 @@ def build():
                             ts(Z, G, 0.0, ALU.max)
                     i += n
                 m = 1 if CFG["msum"][t][s] and l < 2 else 0
-                if not (m and l == 0):
-                    pq = R(Qb, (l - m) * nc, (l + 1) * nc)
+                if how in ("rs", "mx"):
+                    pq, i, ds = dist(l, l + 1), 0, []
+                    for n, how in xs[l]:
+                        if ds and ds[-1][2] == how:
+                            ds[-1][1] += n
+                        else:
+                            ds.append([i, i + n, how])
+                        i += n
+                    ds = [(R(pq[1], pq[4] + a, pq[4] + b), R("nob" if how == "mx" else "pob"), R("dsb", D[4] + a, D[4] + b)) for a, b, how in ds]
+                    xsum = [(pq, R("bn", 15 - d, 143 - d), R("gx", x0 + d, x0 + 16 * nc, 16)) for d in range(16)]
+                    mms(xsum + ds, stop=False)
+                    mms([(pq, R("b2", 15 - d, 143 - d), R("zz", x0 + d, x0 + 16 * nc, 16)) for d in range(16)], start=False)
+                elif not (m and l == 0):
+                    pq = dist(l - m, l + 1)
                     grp = [(pq, R("b2" if half else "b1", 15 - d, 143 - d), R("zz", x0 - 16 * nc * m + d, x0 + 16 * nc, 16)) for d in range(16)]
                     runs, i = [], (l - m) * nc
                     for n, how in [p for j in range(l - m, l + 1) for p in xs[j]]:
@@ -416,9 +471,9 @@ def build():
 
             def near(a, b):
                 if CFG["sign"]:
-                    act(lv("near", a, b), R(Qb, a * nc, b * nc), ACT.Sign, scale=-1.0, bias=R("thf", 1, 2))
+                    act(lv("near", a, b), dist(a, b), ACT.Sign, scale=-1.0, bias=R("thf", 1, 2))
                 else:
-                    ts(lv("near", a, b), R(Qb, a * nc, b * nc), R("thf", 0, 1), ALU.is_le)
+                    ts(lv("near", a, b), dist(a, b), R("thf", 0, 1), ALU.is_le)
 
             def first(a, b):
                 c = -float(V) if CFG["sign"] else -2.0 * V
@@ -445,9 +500,15 @@ def build():
             D = R("dsb", t * CH + c0, t * CH + c1)
             pq = R(Qb, 6 * nc, 7 * nc)
             m = R("mm", t * CH + c0, t * CH + c1)
-            ow, z, pw = R("offw", 8 * s, 8 * s + K), R("zs", c0, c1), R(Pb, 0, nc)
+            ow, z, pw = R("offw", 8 * s, 8 * s + K), R("zs", c0, c1), R(Pb, 7 * nc, 8 * nc)
             h0 = 128 * s + 64
-            hold, pl, es = R("hold", h0, h0 + nc), [] if s == 0 else [(pw, R("nidh"), z)], []
+            hold, pl, es = R("hold", h0, h0 + nc), [] if s == 0 or CFG["cross"] else [(pw, R("nidh"), z)], []
+            for s2, (a, b) in enumerate(STREAMS[:s] if CFG["cross"] else []):
+                for k in range(a // 16, b // 16):
+                    e = R("ex", nc * k, nc * (k + 1))
+                    j = 128 * s2 + 64 + 16 * k - a + 15
+                    ts(e, pq, R("hold", j, j + 1), ALU.is_equal)
+                    es.append((nc, e))
             together()
             tt(m, R(mask, 0, nc), pq, ALU.mult)
             vec("tensor_tensor_scan", hold, R("nmask", 0, nc), m, 0.0, ALU.mult, ALU.add)
@@ -456,11 +517,12 @@ def build():
                 e = R("ee", 4 * c0 + k * nc, 4 * c0 + k * nc + n)
                 tt(e, R("hold", h0 + nc - 16 * k - 1 - n, h0 + nc - 16 * k - 1), R(Qb, 7 * nc - n, 7 * nc), ALU.is_equal)
                 es.append((n, e))
-            pl += [(R(Pb, nc - n, nc), R("o4h"), e) for n, e in es]
+            pl += [(R(Pb, 8 * nc - n, 8 * nc), R("o4h"), e) for n, e in es]
             together(False)
-            if t < RO - 1 or s < NS - 1:
-                pt = R(Pb, 4 * nc, 5 * nc)
-                mms([(pt, R("nidh"), R("ct", 0, nc)), (pt, R("idh"), m)] + [(R(Pb, 5 * nc - n, 5 * nc), R("o4h"), e) for n, e in es])
+            tomb = t < RO - 1 or (s < NS - 1 and not CFG["cross"])
+            if tomb:
+                pt = R(Pb, 8 * nc, 9 * nc)
+                mms([(pt, R("nidh"), R("ct", 0, nc)), (pt, R("idh"), m)] + [(R(Pb, 9 * nc - n, 9 * nc), R("o4h"), e) for n, e in es])
             together()
             ts(ow, R("hold", h0 + 15, h0 + nc, 16), -1.0, ALU.mult, float(V), ALU.add)
             tt(z, IND(xwin, ow), D, ALU.subtract)
@@ -486,7 +548,7 @@ def build():
                     dw = R("cn", t * CH + c0, t * CH + c1)
                 together(False)
                 send(t, R("lande", t * CH + c0, t * CH + c1), dw)
-            if t < RO - 1 or s < NS - 1:
+            if tomb:
                 together()
                 vec("tensor_tensor_scan", R("hold2", c0, c1), R("maskd", c0, c1), pt, 0.0, ALU.min, ALU.max)
                 ot = R("offt", 8 * s, 8 * s + K)
@@ -508,6 +570,7 @@ MODELS = [
     {"f": 1.08, "g": 1.3, "tt": 2.4, "sc": 3.8, "pe": 0.45, "pm": 3, "pl": 120, "sf": 30, "hx": 200, "hs": 110, "ri": 800, "rt": 1300, "rl": 2700, "bw": 450.0, "unit": 62.0},
     {"f": 1.06, "g": 1.4, "tt": 2.6, "sc": 3.8, "pe": 0.49, "pm": 6, "pl": 110, "sf": 80, "hx": 140, "hs": 105, "ri": 600, "rt": 800, "rl": 2850, "bw": 550.0, "unit": 62.0},
     {"f": 1.4, "g": 1.8, "tt": 2.8, "sc": 5.5, "pe": 0.6, "pm": 8, "pl": 120, "sf": 60, "hx": 180, "hs": 160, "ri": 900, "rt": 1300, "rl": 3000, "bw": 500.0, "unit": 82.0},
+    {"f": 1.2, "g": 1.5, "tt": 2.6, "sc": 4.5, "pe": 0.51, "pm": 5, "pl": 120, "sf": 45, "hx": 190, "hs": 130, "ri": 850, "rt": 1300, "rl": 2800, "bw": 470.0, "unit": 70.0},
 ]
 ENG = {"v": 0, "s": 1, "t": 2, "g": 3, "y": 4, None: 5}
 OTHERS = [(1, 2), (0, 2), (0, 1)]
@@ -559,15 +622,21 @@ def replay(tab, order, eng, p0=0, old=None, upto=None):
     tb, hx, hs = tab
     n = len(tb)
     if old is None or p0 < STRIDE:
-        p0, q, fin, bank, dq, lq, why, bl, snaps = 0, [0.0] * 6, [0.0] * n, [-1e9] * 24, 0.0, [-1] * 6, [-1] * n, [-1] * 24, [None]
+        p0, q, bank, dq, lq, bl, snaps = 0, [0.0] * 6, [-1e9] * 24, 0.0, [-1] * 6, [-1] * 24, [None]
+        fin, why = (old[0][:], old[1][:]) if old else ([0.0] * n, [-1] * n)
     else:
         k = p0 // STRIDE
         p0, fin, why, snaps = k * STRIDE, old[0][:], old[1][:], old[2][:k + 1]
         q, bank, lq, bl, dq = snaps[k]
         q, bank, lq, bl = q[:], bank[:], lq[:], bl[:]
-    nxt = p0 + STRIDE
+    nxt, same = p0 + STRIDE, 0
     for p in range(p0, n):
         if p == nxt:
+            if upto is not None and p > upto:
+                o = old[2][len(snaps)]
+                same = same + 1 if o[0] == q and o[1] == bank and o[4] == dq else 0
+                if same == 2:
+                    return fin, why, snaps + old[2][len(snaps):]
             snaps.append((q[:], bank[:], lq[:], bl[:], dq))
             nxt += STRIDE
         i = order[p]
@@ -653,9 +722,15 @@ def schedule(ops):
         x[0] = (x[0] * 1103515245 + 12345) % 2147483648
         return x[0] / 2147483648.0
 
-    def value(o, e, p0, old):
-        res = [replay(t, o, e, p0, old[k] if old else None) for k, (t, u) in enumerate(tabs)]
-        return sum((max(r[0]) + 0.05 * sum(r[0]) / n + sum(w * r[0][i] for i, w in moves)) / u for r, (t, u) in zip(res, tabs)) * 3 / len(tabs), res
+    def value(o, e, p0=0, old=None, upto=None, room=1e9):
+        res, val = [], []
+        for k, (t, u) in enumerate(tabs):
+            r = replay(t, o, e, p0, old[1][k] if old else None, upto)
+            res.append(r)
+            val.append((max(r[0]) + 0.05 * sum(r[0]) / n + sum(w * r[0][i] for i, w in moves)) / u * 3 / len(tabs))
+            if old and sum(val) - sum(old[2][:k + 1]) > room + (2.0 if k + 1 < len(tabs) else 0.0):
+                return None
+        return sum(val), res, val
     moves = [i for i in range(n) if ops[i]["kind"] == "rdma" and ops[i]["ins"][0][1][0][1] != "landd"]
     moves = list(zip(moves, CFG["pull"]))
 
@@ -684,11 +759,13 @@ def schedule(ops):
         a = [y for y in order[lo:hi + 1] if y in carry]
         b = [y for y in order[lo:hi + 1] if y not in carry]
         return order[:lo] + (b + a if d > 0 else a + b) + order[hi + 1:]
-    cur = value(order, eng, 0, None)
+    cur = value(order, eng)
     best, arcs = (cur[0], order, eng), path(cur[1])
     steps = CFG["steps"]
     for it in range(steps):
         o2, e2, r = order, eng, rnd()
+        if it % 512 == 0:
+            cur = value(order, eng)
         if it % 16 == 0:
             arcs = path(cur[1])
         if r < 0.75 and arcs:
@@ -698,27 +775,27 @@ def schedule(ops):
                 i = v if u < 0 or not flex[u] or (flex[v] and rnd() < 0.5) else u
                 e2 = eng[:]
                 e2[i] ^= 1
-                p0 = k = order.index(i)
+                p0 = p1 = k = order.index(i)
                 if rnd() < 0.4:
                     c = [y for y in order[max(0, k - 10):k + 10] if flex[y] and eng[y] == e2[i]]
                     if c:
                         e2[c[int(rnd() * len(c))]] ^= 1
-                    p0 = max(0, k - 10)
+                    p0, p1 = max(0, k - 10), k + 10
             else:
-                p0, kv = order.index(u), order.index(v)
-                o2 = move(kv, p0) if r2 < 0.65 else move(p0, kv)
+                p0, p1 = order.index(u), order.index(v)
+                o2 = move(p1, p0) if r2 < 0.65 else move(p0, p1)
         else:
             k = int(rnd() * n)
             d, j, cnt = (1 if rnd() < 0.5 else -1), k, 1 + int(rnd() ** 2 * 3)
             while cnt and 0 <= j + d < n:
                 j += d
                 cnt -= eng[order[j]] == eng[order[k]]
-            o2, p0 = (None if cnt else move(k, j)), min(k, j)
+            o2, p0, p1 = (None if cnt else move(k, j)), min(k, j), max(k, j)
         if o2 is None:
             continue
-        new = value(o2, e2, p0, cur[1])
         heat = CFG["heat"] * (1 - it / steps) ** 2 + 0.05
-        if new[0] <= cur[0] or rnd() < math.exp((cur[0] - new[0]) / heat):
+        new = value(o2, e2, p0, cur, p1, -heat * math.log(1.0 - rnd()))
+        if new:
             cur, order, eng = new, o2, e2
             arcs = path(cur[1])
             if new[0] < best[0]:

import math
from concourse.mybir import AluOpType as ALU, ActivationFunctionType as ACT

V, HB, CH, RO, N = 2048, 4096, 96, 3, 8
XW = V + 112
FAR = 1024.0
A_, P_ = "abs", "pe"
CFG = {
    "streams": [(0, 48), (48, 96)],
    "banks": [("ps0", "ps1", ["ps4", "ps5"]), ("ps2", "ps3", ["ps6", "ps7"])],
    "lp": [[[[24, 24]] * 3] * 2] * 3,
    "xp": [[[[(24, "mx"), (24, "rs")], [(24, "mx"), (24, "rs")], [(24, "mx"), (24, "mx")]]] * 2] * 3,
    "early": [[1, 1]] * 3, "pre": 1, "sign": 0, "sq": 0, "sint": 0, "gd": 0, "join": 0, "cross": 1, "tab": 0, "cl": 1, "tabfrom": 2, "split": [1, 1],
    "sx": [[[1, 1, 1]] * 2] * 3,
    "msum": [[0, 0]] * 3,
    "dead": [20000, 26500, 33000, 39500, 46000, 52500],
    "win": 300, "seed": 3, "steps": 80000, "heat": 22.0, "pull": [0.3, 0.3, 0.3, 0.2, 0.1, 0.0], "models": [1, 3],
}
MAXS = 3

SCRATCH = {
    "hdw": ("sbuf", [128, HB + 8], "int32"), "nxw": ("sbuf", [128, V + 8], "int32"),
    "xw": ("sbuf", [128, XW], "bfloat16"),
    "c0b": ("sbuf", [128, CH], "bfloat16"), "wtb": ("sbuf", [128, 16], "bfloat16"),
    "thi": ("sbuf", [128, 4], "int32"), "thf": ("sbuf", [128, 4], "float32"),
    "dcol": ("sbuf", [128, 128], "float32"), "gcol": ("sbuf", [128, 128], "float32"),
    "pi": ("sbuf", [128, 8], "int32"), "pf": ("sbuf", [128, 8], "float32"),
    "blk": ("sbuf", [128, 128], "float32"), "deq": ("sbuf", [128, 128], "float32"),
    "tmpa": ("sbuf", [128, 128], "float32"), "tmpb": ("sbuf", [128, 128], "float32"), "tmpc": ("sbuf", [128, 128], "float32"),
    "tmpd": ("sbuf", [128, 128], "float32"),
    "rot": ("sbuf", [128, 128], "bfloat16"), "rott": ("sbuf", [128, 128], "bfloat16"), "wsh": ("sbuf", [128, 128], "bfloat16"),
    "idb": ("sbuf", [128, 128], "bfloat16"), "nidb": ("sbuf", [128, 128], "bfloat16"),
    "idh": ("sbuf", [128, 128], "float16"), "nidh": ("sbuf", [128, 128], "float16"), "n4h": ("sbuf", [128, 128], "float16"),
    "oneh": ("sbuf", [128, 128], "float16"), "trih": ("sbuf", [128, 128], "float16"),
    "o4h": ("sbuf", [128, 128], "float16"), "o4n": ("sbuf", [128, 128], "float16"),
    "base": ("sbuf", [128, 2 * CH], "bfloat16"), "zero": ("sbuf", [128, 2 * CH], "bfloat16"),
    "ed": ("sbuf", [128, 2048], "float16"),
    "b1": ("sbuf", [128, 144], "bfloat16"), "b2": ("sbuf", [128, 144], "bfloat16"), "bn": ("sbuf", [128, 144], "bfloat16"),
    "rio": ("sbuf", [128, 1024], "bfloat16"), "rr": ("sbuf", [128, 1024], "bfloat16"),
    "nmask": ("sbuf", [128, CH], "float32"), "maskd": ("sbuf", [128, CH], "float32"),
    "placed": ("sbuf", [128, CH], "float32"), "ct": ("sbuf", [128, CH], "float16"),
    "g8a": ("sbuf", [128, 8], "float16"), "g8b": ("sbuf", [128, 8], "float16"),
    "c512": ("sbuf", [128, CH], "bfloat16"),
    "landd": ("sbuf", [128, 2 * CH], "bfloat16"), "lande": ("sbuf", [128, 2 * CH], "bfloat16"), "landf": ("sbuf", [128, CH], "float32"),
    "dsb": ("sbuf", [128, RO * CH], "bfloat16"), "dtb": ("sbuf", [128, 128 * MAXS], "bfloat16"),
    "h1": ("sbuf", [128, CH], "int32"), "h2": ("sbuf", [128, CH], "int32"), "h3": ("sbuf", [128, CH], "int32"),
    "h4": ("sbuf", [128, CH], "int32"), "h5": ("sbuf", [128, CH], "int32"), "hu": ("sbuf", [128, CH], "uint16"),
    "off": ("sbuf", [128, 3 * CH], "uint16"), "sl": ("sbuf", [128, 48 * CH], "float16"),
    "cx": ("sbuf", [128, 1024], "float16"), "drep3": ("sbuf", [128, CH, 16], "bfloat16"),
    "gl0": ("sbuf", [128, 16 * CH], "float16"), "gl1": ("sbuf", [128, 16 * CH], "float16"), "gl2": ("sbuf", [128, 16 * CH], "float16"),
    "gx": ("sbuf", [128, 48 * CH], "bfloat16"), "zz": ("sbuf", [128, 48 * CH], "bfloat16"),
    "drep": ("sbuf", [128, 16 * CH], "bfloat16"),
    "near": ("sbuf", [128, 3 * CH], "float16"), "yy": ("sbuf", [128, 3 * CH], "float16"),
    "mm": ("sbuf", [128, RO * CH], "float16"), "hold": ("sbuf", [128, 128 * MAXS], "float32"), "hold2": ("sbuf", [128, CH], "float32"),
    "offw": ("sbuf", [128, 8 * MAXS], "uint16"), "offt": ("sbuf", [128, 8 * MAXS], "uint16"),
    "ee": ("sbuf", [128, 4 * CH], "float16"), "zs": ("sbuf", [128, CH], "float16"), "dl": ("sbuf", [128, CH], "int32"),
    "ww": ("sbuf", [128, RO * CH], "float16"), "dw": ("sbuf", [128, RO * CH], "bfloat16"),
    "hdu": ("sbuf", [128, HB], "float32"), "ua": ("sbuf", [128, 256], "int32"), "ub": ("sbuf", [128, 256], "int32"),
    "uc": ("sbuf", [128, 256], "int32"), "ul": ("sbuf", [128, 256], "uint16"),
    "pob": ("sbuf", [128, 128], "bfloat16"), "nob": ("sbuf", [128, 128], "bfloat16"), "ex": ("sbuf", [128, 4 * CH], "float16"), "cn": ("sbuf", [128, 2 * CH], "bfloat16"), "cf": ("sbuf", [128, CH], "float32"), "yts": ("sbuf", [128, RO * CH], "float32"),
}
for b in range(8):
    SCRATCH["ps%d" % b] = ("psum", [128, 512], "float32")
SEMAPHORES = ["qv", "qs", "qt", "qg", "sent"] + ["d%d" % i for i in range(16)] + ["a%d" % i for i in range(6 * MAXS)]
BYTES = {"float32": 4, "int32": 4, "bfloat16": 2, "float16": 2, "uint16": 2}


def R(name, c0=0, c1=None, step=1, p0=0, p1=128):
    if c1 is None:
        c1 = SCRATCH[name][1][1]
    return ("r", name, p0, p1, c0, c1, step)


def IND(win, off):
    return ("i", win, off)


def isref(a):
    return isinstance(a, tuple) and len(a) > 0 and a[0] in ("r", "i", "d", "3")


def cols(r):
    if r[0] == "i":
        return 16 * cols(r[2])
    if r[0] == "3":
        return (r[5] - r[4]) // 16 * (r[8] - r[7])
    return len(range(r[4], r[5], r[6]))


def width(r):
    return BYTES[SCRATCH[(r[1] if r[0] != "i" else r[1][1])][2]]


def build():
    ops, log, tag, run = [], {}, ["-"], [0]

    def together(on=True):
        run[0] = int(on)
    STREAMS = CFG["streams"]
    NS = len(STREAMS)

    def add(eng, ins, cost, kind="c", after=(), extra=None, alt=None):
        rd, wr = [], []
        for m, args, kw in ins:
            refs = [(i == 0, a) for i, a in enumerate(args) if isref(a)] + [(False, a) for a in kw.values() if isref(a)]
            for out, a in refs:
                if kind == "rdma" and out:
                    continue
                if a[0] == "i":
                    rd.append(a[2])
                    (wr if out else rd).append(a[1])
                elif a[0] != "d":
                    (wr if out else rd).append(a)
        join = run[0] > 1 and CFG["join"]
        run[0] += run[0] > 0
        me = len(ops) - join
        deps = {}
        for isw, lst in ((False, rd), (True, wr)):
            for a in lst:
                for o, ow, b in log.get(a[1], []):
                    if (isw or ow) and a[2] < b[3] and b[2] < a[3] and a[4] < b[5] and b[4] < a[5] and (a[0] != "3" or (a[7] < b[8] and b[7] < a[8])):
                        deps[o] = "ord" if (eng == "t" and ops[o]["eng"] == "t") else "raw"
        for o in after:
            deps.setdefault(o, "ord")
        for isw, lst in ((False, rd), (True, wr)):
            for a in lst:
                if isw and a[6] == 1:
                    log[a[1]] = [x for x in log.get(a[1], []) if not (a[2] <= x[2][2] and x[2][3] <= a[3] and a[4] <= x[2][4] and x[2][5] <= a[5])]
                log.setdefault(a[1], []).append((me, isw, a))
        banks = sorted({a[1] for a in rd + wr if a[1].startswith("ps")})
        forms = {eng: (ins, cost)}
        if alt:
            forms["s"] = alt
        if join:
            op = ops[me]
            wait = [("wait", (), {})] if deps.pop(me, None) else []
            op["forms"] = {e: (i0 + wait + forms[e][0], ("run", c0, forms[e][1], len(wait))) for e, (i0, c0) in op["forms"].items() if e in forms}
            op["ins"], op["cost"] = op["forms"][eng]
            op["deps"].update(deps)
            op["banks"] = sorted(set(op["banks"] + banks))
            return me
        ops.append({"ph": tag[0], "eng": eng, "ins": ins, "cost": cost, "kind": kind, "deps": deps, "banks": banks, "x": extra, "forms": forms})
        return me

    def vec(m, *args, alt=None):
        refs = [a for a in args if isref(a)]
        n = cols(args[0])
        if args[0][0] == "i":
            cost = ("sc", n)
        elif any(a[0] == "i" for a in refs):
            cost = ("gt" if m == "tensor_tensor" else "g", n)
        else:
            big = [a for a in refs if cols(a) == n]
            f = 0.5 if all(width(a) == 2 for a in big) else 1.0
            if m == "tensor_tensor":
                f = 1.0 if any(a[1].startswith("ps") for a in big[1:]) else 2.0
            cost = ("v", n * f)
        return add("v", [(m, args, {})], cost, alt=alt)

    def ts(out, a, s1, op0, s2=None, op1=None, alt=None):
        if tag[0] == "-" and op0 == ALU.mult and op1 in (None, ALU.add):
            alt = actf(out, a, ACT.Identity, scale=s1, bias=0.0 if op1 is None else s2)
        return vec("tensor_scalar", out, a, s1, s2, op0, alt=alt) if op1 is None else vec("tensor_scalar", out, a, s1, s2, op0, op1, alt=alt)

    def tt(out, a, b, op):
        return vec("tensor_tensor", out, a, b, op)

    def actf(out, a, f, **kw):
        return [("activation", (out, a, f), kw)], ("gs" if a[0] == "i" else "s", cols(a))

    def act(out, a, f, **kw):
        return add("s", *actf(out, a, f, **kw))

    def copy(out, a):
        return vec("tensor_copy", out, a, alt=actf(out, a, ACT.Copy))

    inbank, shut = {}, {}

    def mms(lst, start=True, stop=True):
        ins, c = [], 0
        for i, (o, l, r) in enumerate(lst):
            ins.append(("matmul", (o, l, r, start and i == 0, stop and i == len(lst) - 1), {}))
            c += max(min(64, cols(l)), cols(r)) * (4 if width(l) == 4 else 1)
        bank = lst[0][0][1]
        after = list(inbank.get(bank, [])) if start != stop else [shut[bank]] if bank in shut else []
        me = add("t", ins, ("t", c, len(lst)), after=after)
        if start != stop:
            inbank[bank], shut[bank] = [], me
        inbank.setdefault(bank, []).append(me)
        return me

    nd = [0]

    def dma(q, out, in_, nbytes, after=()):
        nd[0] += 1
        return add(q, [("dma_start", (out, in_), {})], ("dma", nbytes), "dma", after, "d%d" % (nd[0] - 1))

    na = [0]

    def send(t, dst, src):
        sem = "a%d" % na[0]
        na[0] += 1
        o = add("g", [("remote", (dst, src), {})], ("r",), "rdma", (), (t, sem))
        return add(None, [("arrive", (dst,), {})], ("a",), "arr", (o,), (t, sem))

    turn = 8 if CFG["sq"] else 0
    a = dma("y", R("c0b"), ("d", "c0", None), 24576)
    a = dma("y", R("hdw", turn, HB + turn), ("d", "hd", None), 128 * HB * 4, (a,))
    for o, i, n in [(R("nxw", 0, V), ("d", "nx", None), 128 * V * 4), (R("xw", 0, V), ("d", "xr", None), 128 * V * 2)][::CFG.get("xf", 1)]:
        a = dma("y", o, i, n, (a,))
    a = dma("s", R("wtb"), ("d", "wt", None), 4096)
    if turn:
        a = dma("s", R("hdw", 0, turn), ("d", "hd", (HB - turn, HB)), 4096, (a,))
    a = dma("s", R("thi", 0, 1), ("d", "th", None), 512, (a,))
    W = 16 * max(b - a for a, b in STREAMS)
    hows = {x[1] for a in CFG["xp"] for b in a for c in b for x in c}
    imp = {"allow_small_or_imprecise_dtypes": True}
    add("g", [("iota", (R("pi", 0, 1), [[0, 1]], 0, 1), {})], ("io", 1))
    add("g", [("iota", (R("gcol"), [[1, 8], [0, 16]], 0, 0), imp)], ("io", 128))
    add("g", [("iota", (R("dcol"), [[0, 8], [1, 16]], 0, 0), imp)], ("io", 128))
    add("g", [("iota", (R("rio", 0, W), [[1, W // 16], [0, 16]], 0, -1), imp)], ("io", W))
    together()
    ts(R("pi", 1, 2), R("pi", 0, 1), 4, ALU.arith_shift_right)
    ts(R("pi", 2, 3), R("pi", 0, 1), 15, ALU.bitwise_and)
    vec("tensor_copy", R("pf", 1, 3), R("pi", 1, 3))
    pg, pd = R("pf", 1, 2), R("pf", 2, 3)
    together()
    ts(R("blk"), R("gcol"), pg, ALU.is_equal)
    ts(R("deq"), R("dcol"), pd, ALU.is_equal)
    copy(R("tmpc", 1, 128), R("deq", 0, 127))
    copy(R("tmpc", 0, 1), R("deq", 127, 128))
    tt(R("rott"), R("tmpc"), R("blk"), ALU.mult)
    together()
    copy(R("tmpa", 0, 127), R("deq", 1, 128))
    copy(R("tmpa", 127, 128), R("deq", 0, 1))
    tt(R("rot"), R("tmpa"), R("blk"), ALU.mult)
    together(False)
    mms([(R("ps7", 0, 16), R("rott"), R("wtb"))])
    together()
    for gq in range(8):
        ts(R("wsh", 16 * gq, 16 * gq + 16), R("ps7", 0, 16), R("blk", 16 * gq, 16 * gq + 1), ALU.mult)
    together()
    tt(R("idh"), R("deq"), R("blk"), ALU.mult)
    ts(R("nidh"), R("idh"), -1.0, ALU.mult)
    for d in range(16 if any(x == 0 for a in CFG["sx"] for b in a for x in b) else 0):
        if d % 4 == 0:
            together()
        ts(R("ed", 128 * d, 128 * d + 128), R("nidh"), R("deq", d, d + 1), ALU.mult)
    together(False)
    ts(R("nidb"), R("idh"), -1.0, ALU.mult)
    if CFG["sign"]:
        copy(R("idb"), R("idh"))
    together()
    copy(R("oneh"), R("blk"))
    ts(R("o4h"), R("oneh"), -4096.0, ALU.mult)
    together()
    ts(R("tmpb"), R("dcol"), pd, ALU.is_gt)
    tt(R("tmpd"), R("tmpb"), R("deq"), ALU.subtract)
    together(False)
    if CFG["sign"]:
        ts(R("o4n"), R("oneh"), -2048.0, ALU.mult)
        for l in range(3):
            ts(R("pf", 4 + l, 5 + l), pd, 16.0 * l, ALU.add, -2048.0, ALU.mult)
            ts(R("base", l * W // 16, (l + 1) * W // 16), R("deq", 0, W // 16), 0.0, ALU.mult, R("pf", 4 + l, 5 + l), ALU.add)
    o4n = R("o4n" if CFG["sign"] else "o4h")
    tt(R("trih"), R("tmpd"), o4n, ALU.mult)
    bs = [("b1", 1.0)] if hows & {"pe", "abs", "rl"} else []
    if "rs" in hows:
        copy(R("pob"), R("blk"))
    if hows & {"rs", "mx"}:
        bs += [("b2", 2.0), ("bn", -1.0)]
        ts(R("nob"), R("blk"), -1.0, ALU.mult)
    if "relu" in hows:
        bs += [("b2", 2.0), ("bn", -1.0)]
    for nm, f in bs:
        together()
        vec("memset", R(nm), 0.0)
        ts(R(nm, 15, 128, 16), R("blk", 0, 128, 16), f, ALU.mult)
    together(False)
    ts(R("rr", 0, W), R("rio", 0, W), 0.0, ALU.is_equal)
    together()
    if any(x for a in CFG["sx"] for b in a for x in b):
        ts(R("tmpa"), R("dcol"), pd, ALU.is_lt, -6144.0, ALU.mult)
        ts(R("tmpc"), R("deq"), 4096.0, ALU.mult)
        tt(R("cx", 0, 128), R("tmpa"), R("tmpc"), ALU.add)
        ts(R("cx", 15, 128, 16), R("cx", 15, 128, 16), -6144.0, ALU.add)
        n, top = 128, 16 * max(x for a in CFG["lp"] for b in a for c in b for x in c)
        while n < top:
            copy(R("cx", n, min(2 * n, top)), R("cx", 0, min(n, top - n)))
            n *= 2
    mask = "deq"
    together()
    ts(R("nmask"), R(mask, 0, CH), -1.0, ALU.mult, 1.0, ALU.add)
    ts(R("g8a"), R("blk", 0, 128, 16), -1.0, ALU.mult)
    ts(R("g8b"), R("blk", 0, 128, 16), -256.0, ALU.mult)
    ts(R("ct"), R("nmask"), 4096.0, ALU.mult, float(V), ALU.add)
    together()
    ts(R("pf", 3, 4), pd, -1.0, ALU.mult, -float(V + 1), ALU.add)
    ts(R("placed"), R("gcol", 0, CH), -16.0, ALU.mult, R("pf", 3, 4), ALU.add)
    tt(R("maskd"), R("placed"), R(mask, 0, CH), ALU.mult)
    together()
    for s in range(NS):
        vec("memset", R("hold", 128 * s, 128 * s + 64), 0.0)
    vec("memset", R("c512"), FAR)
    vec("memset", R("xw", V, XW), FAR)
    vec("memset", R("nxw", V, V + 8), V)
    together(False)
    vec("tensor_copy", R("thf", 0, 1), R("thi", 0, 1))
    if CFG["sign"]:
        ts(R("thf", 1, 2), R("thf", 0, 1), 0.5, ALU.add)
    if CFG["sq"]:
        vec("memset", R("thf", 2, 3), 16.0)

    consts = [i for i, op in enumerate(ops) if op["kind"] == "c"]

    def places(u, a, b, h):
        ts(a, u, 32.0, ALU.add)
        tt(b, u, a, ALU.mult)
        ts(h, b, 5, ALU.arith_shift_right, HB - 1, ALU.bitwise_and)
    if CFG["tab"]:
        add("g", [("iota", (R("ua"), [[16, 256]], 0, 0), {})], ("io", 256))
        ts(R("ua"), R("ua"), pd, ALU.add)
        places(R("ua"), R("ub"), R("uc"), R("ub"))
        vec("tensor_copy", R("ul"), R("ub"))
        n = HB // CFG["tab"]
        for i in range(0, HB, n):
            copy(R("hdu", i, i + n), IND(R("hdw", 0, HB), R("ul", i // 16, (i + n) // 16)))

    xwin = R("xw")
    for t in range(RO):
        for s, (c0, c1) in enumerate(STREAMS):
            nc = c1 - c0
            tag[0] = NS * t + s
            Pb, Qb, zb = CFG["banks"][s]
            NZ = len(zb)
            src = [R("c0b", c0, c1)] if t == 0 else [R(n, (t - 1) * CH + c0, (t - 1) * CH + c1) for n in ("landd", "lande")[1 - CFG["split"][t - 1]:]]
            D = R("dsb", t * CH + c0, t * CH + c1)
            DT = R("dtb", 128 * s, 128 * s + 128, 1, 0, nc)
            ph = R(Pb, 7 * nc, 8 * nc)
            mms([(ph, R("wsh"), x) for x in src])
            pD, pDT = R(Qb, 0, nc), R(Qb, 3 * nc, 3 * nc + 128, 1, 0, nc)
            if not CFG["gd"] or any(h == "pe" for p in CFG["xp"][t][s] for n, h in p):
                mms([(pDT, x, R("rot")) for x in src])
                copy(DT, pDT)
            mms([(pD, R("rot"), x) for x in src])
            copy(D, pD)
            if t < RO - 1 and CFG["split"][t]:
                send(t, R("landd", t * CH + c0, t * CH + c1), D)
            h = [R("h%d" % i, c0, c1) for i in range(1, 6)]
            vec("tensor_copy", h[0], ph)
            together()
            ts(h[1], h[0], HB - 1, ALU.bitwise_and)
            heads = R("hdu") if CFG["tab"] and tag[0] >= CFG["tabfrom"] else R("hdw", 0, HB)
            if heads[1] == "hdw":
                places(*h[1:])
            lb, l0 = "hu", c0
            vec("tensor_copy", R(lb, c0, c1), h[4 if heads[1] == "hdw" else 1])
            together(False)
            w0, n0 = 16 * c0, 3 * c0
            xs = CFG["xp"][t][s]
            nr, i, k = max(sum(n for n, h in p if h not in ("pe", "rs", "mx")) for p in xs), 0, 0
            if CFG["gd"] and nr:
                def rep(j0, j1, a=c0, b=c0 + nr):
                    return ("3", "drep3", 0, 128, 16 * a, 16 * b, 1 if j1 - j0 == 16 else 2, j0, j1)
                for o, x in [(rep(j, j + 1), R("dsb", D[4], D[4] + nr)) for j in range(2)] + [(rep(j, 2 * j), rep(0, j)) for j in (2, 4, 8)]:
                    pat = [[0, nr]] + ([[0, o[8] - o[7]]] if o[8] - o[7] > 1 else [])
                    add("g", [("affine_select", (o, x, pat, ALU.is_ge, 0.0, 0, 0), {})], ("as", cols(o)))
            while i < nr and not CFG["gd"]:
                n = min(nr - i, 32 if nr <= 32 else nr // 2)
                pz = R(zb[k], 0, 16 * n)
                mms([(pz, DT, R("rr", 16 * i, 16 * (i + n), 1, 0, nc))])
                copy(R("drep", w0 + 16 * i, w0 + 16 * (i + n)), pz)
                i, k = i + n, k + 1
            sx, held = CFG["sx"][t][s], {}

            def dist(a, b):
                return R(Pb if a == 2 and CFG["early"][t][s] and xs[2][0][1] in ("rs", "mx") else Qb, a * nc, b * nc)
            for l in range(3):
                gl, i, x0 = "gl%d" % l, 0, 3 * w0 + 16 * nc * l
                for n in CFG["lp"][t][s][l]:
                    G = R(gl, w0 + 16 * i, w0 + 16 * (i + n))
                    o = copy(G, IND(heads if l == 0 else R("nxw"), R(lb, l0 + i, l0 + i + n)))
                    if t == 0 and l == CFG["cl"]:
                        ops[o]["deps"] = {**{c: "ord" for c in consts}, **ops[o]["deps"]}
                    if sx[l]:
                        vec("tensor_tensor_scan", R("sl", x0 + 16 * i, x0 + 16 * (i + n)), G, R("cx", 0, 16 * n), -1.0, ALU.max, ALU.add)
                    i += n
                lb, l0 = "off", 3 * c0 + l * nc
                if sx[l]:
                    ts(R(lb, l0, l0 + nc), R("sl", x0 + 15, x0 + 16 * nc, 16), float(V), ALU.add)
                else:
                    pa = R(Pb, (1 + l) * nc, (2 + l) * nc)
                    mms([(pa, R("ed", 128 * d, 128 * d + 128), R(gl, w0 + d, w0 + 16 * nc, 16)) for d in range(16)])
                    ts(R(lb, l0, l0 + nc), pa, -1.0, ALU.mult)
                    if l == 2 or sx[l + 1]:
                        a = min(j for j in range(l + 1) if not any(sx[j:l + 1]))
                        o, x = R("sl", x0 + 15 - 16 * nc * (l - a), x0 + 16 * nc, 16), R(Pb, (1 + a) * nc, (2 + l) * nc)
                        ts(o, x, -1.0, ALU.mult, -float(V), ALU.add, alt=actf(o, x, ACT.Identity, scale=-1.0, bias=-float(V)))
                i, half = 0, any(how == "relu" for j in range(3) for n, how in xs[j] if j == l or (CFG["msum"][t][s] and j < 2 and l < 2))
                kw = {"scale": 0.5} if half else {}
                for n, how in xs[l]:
                    G, a = R("gx", x0 + 16 * i, x0 + 16 * (i + n)), IND(xwin, R(lb, l0 + i, l0 + i + n))
                    Z = R("zz", G[4], G[5])
                    if how == "mx":
                        copy(G, a)
                        pz = R(zb[i > 0], 0, 16 * n)
                        if held.get(pz[1]) != (i, n):
                            held[pz[1]] = (i, n)
                            mms([(pz, DT, R("rr", 16 * i, 16 * (i + n), 1, 0, nc))])
                        tt(Z, G, pz, ALU.max)
                    elif how in ("pe", "rl", "rs"):
                        copy(G, a)
                        pz = R(zb[i > 0], 0, 16 * n)
                        held[pz[1]] = None
                        two = [(pz, DT, R("rr", 16 * i, 16 * (i + n), 1, 0, nc)), (pz, R("nidb"), G)]
                        if CFG["pre"]:
                            mms(two[:1], stop=False)
                            mms(two[1:], start=False)
                        else:
                            mms(two)
                        if how == "rl":
                            ts(Z, pz, 0.0, ALU.max, alt=actf(Z, pz, ACT.Relu))
                        elif how == "rs":
                            ts(Z, pz, -1.0, ALU.mult, 0.0, ALU.max, alt=actf(Z, pz, ACT.Relu, scale=-1.0))
                        else:
                            act(Z, pz, ACT.Abs, **kw)
                    else:
                        tt(G, a, rep(0, 16, c0 + i, c0 + i + n) if CFG["gd"] else R("drep", w0 + 16 * i, w0 + 16 * (i + n)), ALU.subtract)
                        if how == "abs":
                            act(Z, G, ACT.Abs, **kw)
                        else:
                            ts(Z, G, 0.0, ALU.max)
                    i += n
                m = 1 if CFG["msum"][t][s] and l < 2 else 0
                if how in ("rs", "mx"):
                    pq, i, ds = dist(l, l + 1), 0, []
                    for n, how in xs[l]:
                        if ds and ds[-1][2] == how:
                            ds[-1][1] += n
                        else:
                            ds.append([i, i + n, how])
                        i += n
                    ds = [(R(pq[1], pq[4] + a, pq[4] + b), R("nob" if how == "mx" else "pob"), R("dsb", D[4] + a, D[4] + b)) for a, b, how in ds]
                    xsum = [(pq, R("bn", 15 - d, 143 - d), R("gx", x0 + d, x0 + 16 * nc, 16)) for d in range(16)]
                    mms(xsum + ds, stop=False)
                    mms([(pq, R("b2", 15 - d, 143 - d), R("zz", x0 + d, x0 + 16 * nc, 16)) for d in range(16)], start=False)
                elif not (m and l == 0):
                    pq = dist(l - m, l + 1)
                    grp = [(pq, R("b2" if half else "b1", 15 - d, 143 - d), R("zz", x0 - 16 * nc * m + d, x0 + 16 * nc, 16)) for d in range(16)]
                    runs, i = [], (l - m) * nc
                    for n, how in [p for j in range(l - m, l + 1) for p in xs[j]]:
                        if how == "relu":
                            if runs and runs[-1][1] == i:
                                runs[-1][1] = i + n
                            else:
                                runs.append([i, i + n])
                        i += n
                    for a, b in runs:
                        grp += [(R(Qb, a, b), R("bn", 15 - d, 143 - d), R("gx", 3 * w0 + 16 * a + d, 3 * w0 + 16 * b, 16)) for d in range(16)]
                    mms(grp)

            def lv(name, a, b):
                return R(name, n0 + a * nc, n0 + b * nc)

            def pv(a, b):
                return R(Pb, 5 * nc, 6 * nc) if a == 2 else R(Qb, (3 + a) * nc, (3 + b) * nc)

            def cand(a, b):
                c = [(pv(a, b), R("nidh"), R("sl", 3 * w0 + 16 * nc * a + 15, 3 * w0 + 16 * nc * b, 16))]
                return c + ([(pv(a, b), R("idb"), R("base", a * nc, b * nc))] if CFG["sign"] else [])

            def near(a, b):
                if CFG["sign"]:
                    act(lv("near", a, b), dist(a, b), ACT.Sign, scale=-1.0, bias=R("thf", 1, 2))
                else:
                    ts(lv("near", a, b), dist(a, b), R("thf", 0, 1), ALU.is_le)

            def first(a, b):
                c = -float(V) if CFG["sign"] else -2.0 * V
                ts(lv("yy", a, b), pv(a, b), c, ALU.add, 0.0, ALU.max, alt=actf(lv("yy", a, b), pv(a, b), ACT.Relu, bias=c))
            if CFG["early"][t][s]:
                near(0, 2)
                mms(cand(0, 2) + [(pv(1, 2), o4n, lv("near", 0, 1)), (pv(0, 2), R("trih"), lv("near", 0, 2))])
                first(0, 2)
                mms(cand(2, 3) + [(pv(2, 3), o4n, lv("near", l, l + 1)) for l in range(2)], stop=False)
                near(2, 3)
                mms([(pv(2, 3), R("trih"), lv("near", 2, 3))], start=False)
                first(2, 3)
            else:
                near(0, 3)
                mms(cand(0, 3) + [(pv(1, 3), o4n, lv("near", 0, 2)), (R(Qb, 5 * nc, 6 * nc), o4n, lv("near", 0, 1)),
                                  (pv(0, 3), R("trih"), lv("near", 0, 3))])
                first(0, 3)
            mms([(R(Qb, 6 * nc, 7 * nc), R("oneh"), lv("yy", l, l + 1)) for l in range(3)])
        for s, (c0, c1) in enumerate(STREAMS):
            nc = c1 - c0
            tag[0] = NS * t + s
            K = nc // 16
            Pb, Qb, zb = CFG["banks"][s]
            D = R("dsb", t * CH + c0, t * CH + c1)
            pq = R(Qb, 6 * nc, 7 * nc)
            m = R("mm", t * CH + c0, t * CH + c1)
            ow, z, pw = R("offw", 8 * s, 8 * s + K), R("zs", c0, c1), R(Pb, 7 * nc, 8 * nc)
            h0 = 128 * s + 64
            hold, pl, es = R("hold", h0, h0 + nc), [] if s == 0 or CFG["cross"] else [(pw, R("nidh"), z)], []
            for s2, (a, b) in enumerate(STREAMS[:s] if CFG["cross"] else []):
                for k in range(a // 16, b // 16):
                    e = R("ex", nc * k, nc * (k + 1))
                    j = 128 * s2 + 64 + 16 * k - a + 15
                    ts(e, pq, R("hold", j, j + 1), ALU.is_equal)
                    es.append((nc, e))
            together()
            tt(m, R(mask, 0, nc), pq, ALU.mult)
            vec("tensor_tensor_scan", hold, R("nmask", 0, nc), m, 0.0, ALU.mult, ALU.add)
            for k in range(K - 1, -1, -1):
                n = nc if k == K - 1 else nc - 16 * k - 1
                e = R("ee", 4 * c0 + k * nc, 4 * c0 + k * nc + n)
                tt(e, R("hold", h0 + nc - 16 * k - 1 - n, h0 + nc - 16 * k - 1), R(Qb, 7 * nc - n, 7 * nc), ALU.is_equal)
                es.append((n, e))
            pl += [(R(Pb, 8 * nc - n, 8 * nc), R("o4h"), e) for n, e in es]
            together(False)
            tomb = t < RO - 1 or (s < NS - 1 and not CFG["cross"])
            if tomb:
                pt = R(Pb, 8 * nc, 9 * nc)
                mms([(pt, R("nidh"), R("ct", 0, nc)), (pt, R("idh"), m)] + [(R(Pb, 9 * nc - n, 9 * nc), R("o4h"), e) for n, e in es])
            together()
            ts(ow, R("hold", h0 + 15, h0 + nc, 16), -1.0, ALU.mult, float(V), ALU.add)
            tt(z, IND(xwin, ow), D, ALU.subtract)
            together(s == 0)
            run[0] *= 2
            dl = R("dl", c0, c1)
            ts(dl, z, 0.25, ALU.mult, -0.375, ALU.add)
            together(False)
            mms(pl)
            w = R("ww", t * CH + c0, t * CH + c1)
            together()
            ts(w, pw, -256.0, ALU.is_gt)
            dw = R("dw", t * CH + c0, t * CH + c1)
            tt(dw, dl, w, ALU.mult)
            if t == RO - 1:
                tt(R("cf", c0, c1), dw, D, ALU.add)
                together(False)
                send(t, R("landf", c0, c1), R("cf", c0, c1))
                dma("y", ("d", "yc", (c0, c1)), R("landf", c0, c1), 128 * nc * 4)
            else:
                if not CFG["split"][t]:
                    tt(R("cn", t * CH + c0, t * CH + c1), dw, D, ALU.add)
                    dw = R("cn", t * CH + c0, t * CH + c1)
                together(False)
                send(t, R("lande", t * CH + c0, t * CH + c1), dw)
            if tomb:
                together()
                vec("tensor_tensor_scan", R("hold2", c0, c1), R("maskd", c0, c1), pt, 0.0, ALU.min, ALU.max)
                ot = R("offt", 8 * s, 8 * s + K)
                ts(ot, R("hold2", c0 + 15, c1, 16), -1.0, ALU.mult)
                together(False)
                vec("tensor_copy", IND(xwin, ot), R("c512", 0, nc))
    tag[0] = "e"
    yb = CFG["banks"][0][2][0]
    for t in range(RO):
        o = R(yb, t * CH, (t + 1) * CH, 1, 0, 8)
        mms([(o, R("g8a"), R("mm", t * CH, (t + 1) * CH)), (o, R("g8b"), R("ww", t * CH, (t + 1) * CH))])
    ts(R("yts", 0, RO * CH, 1, 0, 8), R(yb, 0, RO * CH, 1, 0, 8), 6144.0, ALU.add, float(V), ALU.min)
    dma("s", ("d", "yt", None), R("yts", 0, RO * CH, 1, 0, 8), 8 * RO * CH * 4)
    return ops


MODELS = [
    {"f": 1.06, "g": 1.2, "tt": 2.4, "sc": 3.0, "pe": 0.5, "pm": 0, "pl": 100, "sf": 30, "hx": 170, "hs": 70, "ri": 900, "rt": 1100, "rl": 2300, "bw": 450.0, "unit": 58.0},
    {"f": 1.08, "g": 1.3, "tt": 2.4, "sc": 3.8, "pe": 0.45, "pm": 3, "pl": 120, "sf": 30, "hx": 200, "hs": 110, "ri": 800, "rt": 1300, "rl": 2700, "bw": 450.0, "unit": 62.0},
    {"f": 1.06, "g": 1.4, "tt": 2.6, "sc": 3.8, "pe": 0.49, "pm": 6, "pl": 110, "sf": 80, "hx": 140, "hs": 105, "ri": 600, "rt": 800, "rl": 2850, "bw": 550.0, "unit": 62.0},
    {"f": 1.4, "g": 1.8, "tt": 2.8, "sc": 5.5, "pe": 0.6, "pm": 8, "pl": 120, "sf": 60, "hx": 180, "hs": 160, "ri": 900, "rt": 1300, "rl": 3000, "bw": 500.0, "unit": 82.0},
    {"f": 1.2, "g": 1.5, "tt": 2.6, "sc": 4.5, "pe": 0.51, "pm": 5, "pl": 120, "sf": 45, "hx": 190, "hs": 130, "ri": 850, "rt": 1300, "rl": 2800, "bw": 470.0, "unit": 70.0},
]
ENG = {"v": 0, "s": 1, "t": 2, "g": 3, "y": 4, None: 5}
OTHERS = [(1, 2), (0, 2), (0, 1)]
STRIDE = 24


def times(c, m):
    k = c[0]
    if k == "run":
        d = times(c[1], m)[0] + times(c[2], m)[0] + c[3] * m["hs"]
    elif k in ("v", "s"):
        d = max(64, c[1]) * 0.83 * m["f"] + (m["sf"] if k == "s" else 0)
    elif k == "g":
        d = (50 + c[1] * m["g"] * 0.83) * m["f"]
    elif k == "gt":
        d = (50 + c[1] * max(m["g"], m.get("tt", 1.8)) * 0.83) * m["f"]
    elif k == "gs":
        d = (65 + c[1] * m["g"] * 0.83) * m["f"] + m["sf"]
    elif k == "sc":
        d = (50 + c[1] * m["sc"] * 0.83) * m["f"]
    elif k == "t":
        d = c[1] * m["pe"] + c[2] * m["pm"]
        return d, d + m["pl"]
    elif k == "io":
        d = (130 + 2 * c[1] * 0.83) * m["f"]
    elif k == "as":
        d = (170 + 2 * c[1] * 0.83) * m["f"]
    elif k == "dma":
        return 60, 1600
    elif k == "r":
        return m["ri"], m["ri"]
    else:
        return 0, m["rl"] - m["ri"] - m["rt"]
    return d, d


def table(ops, m):
    tb = []
    for op in ops:
        cc = [o for o, k in op["deps"].items() if k != "ord" and ops[o]["kind"] == "c" and op["kind"] == "c"]
        xx = [(o, 0 if k == "ord" else m["hx"]) for o, k in op["deps"].items() if o not in cc and (k != "ord" or op["eng"] is None)]
        tb.append(({ENG[e]: times(f[1], m) for e, f in op["forms"].items()},
                   op["cost"][1] / m["bw"] if op["kind"] == "dma" and op["cost"][1] > 30000 else m["rt"] if op["kind"] == "rdma" else -1, cc, xx,
                   [3 * int(b[2]) for b in op["banks"]]))
    return tb, m["hx"], m["hs"]


def replay(tab, order, eng, p0=0, old=None, upto=None):
    tb, hx, hs = tab
    n = len(tb)
    if old is None or p0 < STRIDE:
        p0, q, bank, dq, lq, bl, snaps = 0, [0.0] * 6, [-1e9] * 24, 0.0, [-1] * 6, [-1] * 24, [None]
        fin, why = (old[0][:], old[1][:]) if old else ([0.0] * n, [-1] * n)
    else:
        k = p0 // STRIDE
        p0, fin, why, snaps = k * STRIDE, old[0][:], old[1][:], old[2][:k + 1]
        q, bank, lq, bl, dq = snaps[k]
        q, bank, lq, bl = q[:], bank[:], lq[:], bl[:]
    nxt, same = p0 + STRIDE, 0
    for p in range(p0, n):
        if p == nxt:
            if upto is not None and p > upto:
                o = old[2][len(snaps)]
                same = same + 1 if o[0] == q and o[1] == bank and o[4] == dq else 0
                if same == 2:
                    return fin, why, snaps + old[2][len(snaps):]
            snaps.append((q[:], bank[:], lq[:], bl[:], dq))
            nxt += STRIDE
        i = order[p]
        fm, dm, cc, xx, bk = tb[i]
        e = eng[i]
        s, w = q[e], lq[e]
        for o in cc:
            x = fin[o] + (hs if eng[o] == e else hx)
            if x > s:
                s, w = x, o
        for o, d in xx:
            x = fin[o] + d
            if x > s:
                s, w = x, o
        hold, lat = fm[e]
        if bk:
            for b in bk:
                for e2 in OTHERS[e]:
                    x = bank[b + e2] + hx
                    if x > s:
                        s, w = x, bl[b + e2]
            for b in bk:
                bank[b + e], bl[b + e] = s + lat, i
        f = s + lat
        if dm >= 0:
            f = dq = max(f, dq) + dm
        fin[i], why[i] = f, w
        if e < 5:
            q[e], lq[e] = s + hold, i
    return fin, why, snaps


def first_order(ops, succ):
    n = len(ops)
    tb, hx, hs = table(ops, MODELS[1])
    due, dead = [0.0] * n, CFG["dead"]
    for i in range(n - 1, -1, -1):
        d = min([due[j] - hx for j in succ[i]], default=dead[-1] + 4000)
        if ops[i]["kind"] == "rdma" and ops[i]["ins"][0][1][0][1] != "landd":
            d = min(d, dead[ops[i]["ph"]])
        due[i] = d - min(v[1] for v in tb[i][0].values()) - max(tb[i][1], 0)
    q, fin, bank, dq, eng = [0.0] * 6, [0.0] * n, [-1e9] * 24, 0.0, [5] * n
    left = [len(op["deps"]) for op in ops]
    ready, order = [i for i in range(n) if left[i] == 0], []

    def start(i, e):
        fm, dm, cc, xx, bk = tb[i]
        return max([q[e]] + [fin[o] + (hs if eng[o] == e else hx) for o in cc] + [fin[o] + d for o, d in xx]
                   + [bank[b + e2] + hx for b in bk for e2 in OTHERS[e]])
    while ready:
        ss = [min((start(i, e) + f[1], start(i, e), i, e) for e, f in tb[i][0].items())[1:] for i in ready]
        s0, i0, e0 = min(ss)
        s, i, e = min([c for c in ss if c[0] <= s0 + CFG["win"] and c[2] == e0], key=lambda c: due[c[1]] + 2 * (c[0] - s0))
        fm, dm, cc, xx, bk = tb[i]
        fin[i], eng[i] = s + fm[e][1], e
        if dm >= 0:
            fin[i] = dq = max(fin[i], dq) + dm
        if e < 5:
            q[e] = s + fm[e][0]
        for b in bk:
            bank[b + e] = fin[i]
        order.append(i)
        ready.remove(i)
        for j in succ[i]:
            left[j] -= 1
            if left[j] == 0:
                ready.append(j)
    return order, eng


def schedule(ops):
    n = len(ops)
    succ = [set() for i in range(n)]
    for i, op in enumerate(ops):
        for o in op["deps"]:
            succ[o].add(i)
    order, eng = CFG.get("init", first_order)(ops, succ)
    tabs = [(table(ops, MODELS[k]), MODELS[k]["unit"]) for k in CFG["models"]]
    flex = [len(op["forms"]) > 1 for op in ops]
    x = [CFG["seed"]]

    def rnd():
        x[0] = (x[0] * 1103515245 + 12345) % 2147483648
        return x[0] / 2147483648.0

    def value(o, e, p0=0, old=None, upto=None, room=1e9):
        res, val = [], []
        for k, (t, u) in enumerate(tabs):
            r = replay(t, o, e, p0, old[1][k] if old else None, upto)
            res.append(r)
            val.append((max(r[0]) + 0.05 * sum(r[0]) / n + sum(w * r[0][i] for i, w in moves)) / u * 3 / len(tabs))
            if old and sum(val) - sum(old[2][:k + 1]) > room + (2.0 if k + 1 < len(tabs) else 0.0):
                return None
        return sum(val), res, val
    moves = [i for i in range(n) if ops[i]["kind"] == "rdma" and ops[i]["ins"][0][1][0][1] != "landd"]
    moves = list(zip(moves, CFG["pull"]))

    def path(res):
        arcs = []
        for f, why, sn in res:
            i = f.index(max(f)) if rnd() < 0.5 else moves[int(rnd() * len(moves))][0]
            while why[i] >= 0:
                if i not in succ[why[i]]:
                    arcs.append((why[i], i))
                elif flex[i]:
                    arcs.append((-1, i))
                i = why[i]
        return arcs

    def move(k, j):
        d = 1 if j > k else -1
        carry = [order[k]]
        for p in range(k + d, j + d, d):
            y = order[p]
            if any(y in succ[c] for c in carry) if d > 0 else any(c in succ[y] for c in carry):
                carry.append(y)
        if order[j] in carry:
            return None
        lo, hi = min(j, k), max(j, k)
        a = [y for y in order[lo:hi + 1] if y in carry]
        b = [y for y in order[lo:hi + 1] if y not in carry]
        return order[:lo] + (b + a if d > 0 else a + b) + order[hi + 1:]
    cur = value(order, eng)
    best, arcs = (cur[0], order, eng), path(cur[1])
    steps = CFG["steps"]
    for it in range(steps):
        o2, e2, r = order, eng, rnd()
        if it % 512 == 0:
            cur = value(order, eng)
        if it % 16 == 0:
            arcs = path(cur[1])
        if r < 0.75 and arcs:
            u, v = arcs[int(rnd() * len(arcs))]
            r2 = rnd()
            if u < 0 or (r2 < 0.3 and (flex[u] or flex[v])):
                i = v if u < 0 or not flex[u] or (flex[v] and rnd() < 0.5) else u
                e2 = eng[:]
                e2[i] ^= 1
                p0 = p1 = k = order.index(i)
                if rnd() < 0.4:
                    c = [y for y in order[max(0, k - 10):k + 10] if flex[y] and eng[y] == e2[i]]
                    if c:
                        e2[c[int(rnd() * len(c))]] ^= 1
                    p0, p1 = max(0, k - 10), k + 10
            else:
                p0, p1 = order.index(u), order.index(v)
                o2 = move(p1, p0) if r2 < 0.65 else move(p0, p1)
        else:
            k = int(rnd() * n)
            d, j, cnt = (1 if rnd() < 0.5 else -1), k, 1 + int(rnd() ** 2 * 3)
            while cnt and 0 <= j + d < n:
                j += d
                cnt -= eng[order[j]] == eng[order[k]]
            o2, p0, p1 = (None if cnt else move(k, j)), min(k, j), max(k, j)
        if o2 is None:
            continue
        heat = CFG["heat"] * (1 - it / steps) ** 2 + 0.05
        new = value(o2, e2, p0, cur, p1, -heat * math.log(1.0 - rnd()))
        if new:
            cur, order, eng = new, o2, e2
            arcs = path(cur[1])
            if new[0] < best[0]:
                best = (new[0], o2, e2)
    return best


def plan():
    ops = build()
    v, order, eng = schedule(ops)
    for op, e in zip(ops, eng):
        if len(op["forms"]) > 1:
            op["eng"] = "vs"[e]
            op["ins"], op["cost"] = op["forms"][op["eng"]]
    place_of = {o: k for k, o in enumerate(order)}
    pos, cnt = {}, {}
    known = {e: {} for e in "vstgy"}
    clock, bank, waits, need = {}, {}, {}, set()
    for i in order:
        op = ops[i]
        e = op["eng"]
        if e is None:
            clock[i] = {("x", i): 1}
            continue
        want = {o for o, k in op["deps"].items() if k != "ord"}
        for b in op["banks"]:
            for e2, o in bank.get(b, {}).items():
                if e2 != e:
                    want.add(o)
            bank.setdefault(b, {})[e] = i
        kn, ws = known[e], []
        for o in sorted(want, key=lambda o: -place_of[o]):
            key, val = pos[o] if o in pos else (("x", o), 1)
            if kn.get(key, 0) < val:
                ws.append(o)
                need.add(o)
                for k2, v2 in clock[o].items():
                    if kn.get(k2, 0) < v2:
                        kn[k2] = v2
        waits[i] = ws
        clock[i] = dict(kn)
        if op["kind"] == "c":
            cnt[e] = cnt.get(e, 0) + 1
            pos[i] = (e, cnt[e])
            clock[i][e] = cnt[e]
        else:
            clock[i][("x", i)] = 1
    return ops, order, waits, need, eng


PLAN = []


def rank_program(g, core, T, topo):
    rank = T.rank_of(core)
    if rank is None:
        return
    if not PLAN:
        PLAN.append(plan())
    ops, order, waits, need, eng = PLAN[0]
    dst = [T.cores[(rank + 1 + t % (N - 1)) % N] for t in range(RO)]
    src = [T.cores[(rank - 1 - t % (N - 1)) % N] for t in range(RO)]

    def lanes(a):
        r = T.rank_of(a)
        m = -1
        for t in range(RO):
            m &= topo.mask(a, T.cores[(r + 1 + t % (N - 1)) % N])
        return m
    Q = {"v": g.vector, "s": g.scalar, "t": g.tensor, "g": g, "y": g.sync}

    def A(a):
        if not isref(a):
            return a
        if a[0] == "i":
            return A(a[1]).indirect(A(a[2]))
        if a[0] == "d":
            return T[a[1]][:] if a[2] is None else T[a[1]][:, a[2][0]:a[2][1]]
        if a[0] == "3":
            return T[a[1]][:, a[4] // 16:a[5] // 16, a[7] if a[8] - a[7] == 1 else slice(a[7], a[8])]
        if a[6] == 1:
            return T[a[1]][a[2]:a[3], a[4]:a[5]]
        return T[a[1]][a[2]:a[3], a[4]:a[5]:a[6]]
    at, cnt, sent, last = {}, {}, 0, []
    for i in order:
        op = ops[i]
        e = op["eng"]
        if e is None:
            at[i] = (op["x"][1], bin(lanes(src[op["x"][0]])).count("1"))
            continue
        q = Q[e]
        for o in waits[i]:
            q.wait_ge(T.sem[at[o][0]], at[o][1])
        if op["kind"] == "rdma":
            t, sem = op["x"]
            rid, pid = topo.addr(dst[t])[:2]
            a = op["ins"][0][1]
            g.remote_dma(A(a[0]), A(a[1]), T.sem[sem], T.sem["sent"], pid, rid, lanes(core))
            sent += bin(lanes(core)).count("1")
            continue
        for m, args, kw in op["ins"]:
            if m == "wait":
                cnt[e] = cnt.get(e, 0) + 1
                ins.then_inc(T.sem["q" + e], 1)
                q.wait_ge(T.sem["q" + e], cnt[e])
                continue
            ins = CALL[m](q, [A(x) for x in args], {n: A(x) for n, x in kw.items()})
        if op["kind"] == "dma":
            ins.then_inc(T.sem[op["x"]], 16)
            at[i] = (op["x"], 16)
            if i not in need:
                last.append((q, op["x"]))
        elif i in need:
            cnt[e] = cnt.get(e, 0) + 1
            ins.then_inc(T.sem["q" + e], 1)
            at[i] = ("q" + e, cnt[e])
    g.wait_ge(T.sem["sent"], sent)
    for q, sem in last:
        q.wait_ge(T.sem[sem], 16)


CALL = {
    "matmul": lambda q, a, k: q.matmul(*a),
    "activation": lambda q, a, k: q.activation(*a, **k),
    "tensor_copy": lambda q, a, k: q.tensor_copy(*a),
    "tensor_tensor": lambda q, a, k: q.tensor_tensor(*a),
    "tensor_scalar": lambda q, a, k: q.tensor_scalar(*a),
    "tensor_tensor_scan": lambda q, a, k: q.tensor_tensor_scan(*a),
    "memset": lambda q, a, k: q.memset(*a),
    "iota": lambda q, a, k: q.iota(*a, **k),
    "affine_select": lambda q, a, k: q.affine_select(*a),
    "dma_start": lambda q, a, k: q.dma_start(*a),
}
